import numpy as np
import ml_dtypes


def mxq(x, axis, fmt="e4m3"):
    dtype, down = {"e4m3": (ml_dtypes.float8_e4m3fn, 7), "e5m2": (ml_dtypes.float8_e5m2, 14)}[fmt]
    v = np.moveaxis(np.asarray(x, np.float32).astype(ml_dtypes.bfloat16).astype(np.float64), axis, -1)
    blocks = v.reshape(v.shape[:-1] + (-1, 32))
    amax = np.abs(blocks).max(-1, keepdims=True)
    byte = np.maximum(np.where(amax > 0, np.frexp(amax)[1] - 1 + 127, 0) - down, 1)
    scale = np.exp2(byte - 127.0)
    codes = (blocks / scale).astype(np.float32).astype(dtype).astype(np.float64)
    return np.moveaxis((codes * scale).reshape(v.shape), -1, axis)


WIDE = False


def mx_kscale(k):
    if not WIDE:
        return np.ones(k)
    levels = np.array([10, -10, 5, -5, 0])
    if k % 512:
        return np.exp2(np.random.permutation(np.resize(levels, k // 32))).repeat(32)
    a = np.empty((k // 512, 16))
    for p in range(k // 512):
        a[p, :8] = np.random.permutation(np.resize(levels, 8))
        for g in range(8):
            far = levels[np.abs(levels - a[p, g]) >= 10]
            a[p, g + 8] = far[np.random.randint(len(far))]
    return np.exp2(a.ravel()).repeat(32)


def f64(x):
    return np.asarray(x).astype(np.float64)


def striped(idx):
    return np.tile(idx.reshape(-1, 16).T, (8, 1)).astype(np.uint16)


def unstriped(offs):
    return offs[:16].T.reshape(-1).astype(np.int64)

def planes(y):
    n, m = y.shape
    v = y.astype(np.float32).astype(ml_dtypes.bfloat16).astype(np.float64).reshape(n // 32, 32, m)
    top = np.abs(v).max(1)
    byte = np.clip(np.where(top > 0, np.frexp(top)[1] - 1 + 127 - 7, 1), 1, 254)
    codes = (v * np.exp2(127.0 - byte)[:, None, :]).reshape(n, m).astype(np.float32).astype(ml_dtypes.float8_e4m3fn).view(np.uint8)
    words = codes.reshape(n // 512, 128, 4, m).transpose(0, 1, 3, 2)
    return np.ascontiguousarray(words), np.ascontiguousarray(byte.astype(np.uint8).reshape(n // 512, 16, m))


K, T, S, N, U = 512, 1024, 512, 512, 1024


def setup_inputs():
    n = np.random.standard_normal
    s = mx_kscale(K)[:, None]
    return {
        "xT": (n((K, T)) * s).astype(np.float32),
        "mem": n((N, U)).astype(np.float32),
        "w1": (n((K, N)) / np.sqrt(K) / s).astype(np.float32),
        "offs": striped(np.random.permutation(T)[:S]),
        "slot": striped(np.random.permutation(U)[:S]),
    }


def reference(xT, mem, w1, offs, slot):
    xq = mxq(f64(xT)[:, unstriped(offs)], 0, "e4m3")
    y = mxq(f64(w1), 0, "e4m3").T @ xq
    out = f64(mem).copy()
    out[:, unstriped(slot)] = np.minimum(f64(mem)[:, unstriped(slot)], y)
    return (out,) + planes(out)

@@ -1,0 +1,136 @@
+from contextlib import ExitStack
+
+import concourse.mybir as mybir
+
+K, T, S, N, U = 512, 1024, 512, 512, 1024
+FLOPS = 2 * K * S * N
+
+F32 = mybir.dt.float32
+BF16 = mybir.dt.bfloat16
+U32 = mybir.dt.uint32
+I32 = mybir.dt.int32
+U16 = mybir.dt.uint16
+U8 = mybir.dt.uint8
+FP8X4 = mybir.dt.float8_e4m3fn_x4
+MIN = mybir.AluOpType.min
+
+P = 128
+PACK = 4
+CH = 256
+NCH = U // CH
+VCH = 2
+
+
+def tile_picked_idxput_min_lo_kernel(tc, xT, mem, w1, offs, slot, out_0, out_1, out_2):
+    nc = tc.nc
+    with ExitStack() as ctx:
+        sb = ctx.enter_context(tc.tile_pool(name="sb", bufs=1))
+        ps = ctx.enter_context(tc.psum_pool(name="ps", bufs=1))
+
+        offs_t = sb.tile([P, S // 16], U16, name="offs_t")
+        slot_t = sb.tile([P, S // 16], U16, name="slot_t")
+        x_rows = xT.rearrange("(p j) c -> p j c", j=PACK)
+        w_rows = w1.rearrange("(p j) c -> p j c", j=PACK)
+        mem_rows = mem.rearrange("(p t) c -> p t c", t=PACK)
+        out_rows = out_0.rearrange("(p t) c -> p t c", t=PACK)
+
+        x = [sb.tile([P, T], F32, name="x%d" % j) for j in range(PACK)]
+        w = [sb.tile([P, PACK, N // 2], F32, name="w%d" % h) for h in range(2)]
+        win = [sb.tile([P, U], F32, name="win%d" % t) for t in range(PACK)]
+
+        nc.sync.dma_start(offs_t[:], offs)
+        for j in range(PACK):
+            nc.sync.dma_start(x[j][:], x_rows[:, j, :])
+        for h in range(2):
+            nc.sync.dma_start(w[h][:], w_rows[:, :, h * (N // 2) : (h + 1) * (N // 2)])
+        nc.sync.dma_start(slot_t[:], slot)
+        for t in range(PACK):
+            nc.sync.dma_start(win[t][:], mem_rows[:, t, :])
+
+        xg = sb.tile([P, PACK, S], BF16, name="xg", align_bytes=64)
+        for j in range(PACK):
+            nc.vector.tensor_copy(xg[:, j, :], x[j][:].indirect(offs_t[:]))
+        xi = sb.tile([P, S, PACK], BF16, name="xi", align_bytes=64)
+        nc.vector.tensor_copy(
+            xi[:].rearrange("p (c i) j -> p c j i", i=4), xg[:].rearrange("p j (c i) -> p c j i", i=4)
+        )
+        x_codes = sb.tile([P, S], U32, name="x_codes", align_bytes=64)
+        x_scales = sb.tile([P, S], U8, name="x_scales", align_bytes=64)
+        nc.vector.quantize_mx(x_codes[:].bitcast(FP8X4), x_scales[:], xi[:].rearrange("p c j -> p (c j)"))
+
+        w_first = sb.tile([P, P, PACK], BF16, name="w_first", align_bytes=64)
+        w_rest = sb.tile([P, PACK - 1, P, PACK], BF16, name="w_rest", align_bytes=64)
+        for h in range(2):
+            src = w[h][:].rearrange("p j (m t) -> p m t j", t=PACK)
+            ms = slice(h * (P // 2), (h + 1) * (P // 2))
+            nc.scalar.copy(w_first[:, ms, :], src[:, :, 0, :])
+            nc.scalar.copy(w_rest[:, :, ms, :].rearrange("p t m j -> p m t j"), src[:, :, 1:, :])
+        w_codes = [sb.tile([P, P], U32, name="w_codes%d" % t, align_bytes=64) for t in range(PACK)]
+        w_scales = [sb.tile([P, P], U8, name="w_scales%d" % t, align_bytes=64) for t in range(PACK)]
+        y = [ps.tile([P, S], F32, name="y%d" % t) for t in range(PACK)]
+        old = [sb.tile([P, S], F32, name="old%d" % t) for t in range(PACK)]
+        new = [sb.tile([P, S], F32, name="new%d" % t) for t in range(PACK)]
+        grouped = [sb.tile([P, CH, PACK], BF16, name="grouped%d" % c, align_bytes=64) for c in range(NCH)]
+
+        def product(t):
+            src = w_first[:] if t == 0 else w_rest[:, t - 1, :, :]
+            nc.vector.quantize_mx(w_codes[t][:].bitcast(FP8X4), w_scales[t][:], src.rearrange("p m j -> p (m j)"))
+            nc.tensor.matmul_mx(
+                y[t][:], w_codes[t][:].bitcast(FP8X4), w_scales[t][:], x_codes[:].bitcast(FP8X4), x_scales[:],
+                start=True, stop=True,
+            )
+
+        def gather(t):
+            nc.vector.tensor_copy(old[t][:], win[t][:].indirect(slot_t[:]))
+
+        def smaller(t):
+            nc.vector.tensor_tensor(new[t][:], y[t][:], old[t][:], MIN)
+
+        def scatter(t):
+            nc.vector.tensor_copy(win[t][:].indirect(slot_t[:]), new[t][:])
+            nc.sync.dma_start(out_rows[:, t, :], win[t][:])
+
+        def regroup(t, c, engine_copy):
+            engine_copy(grouped[c][:, :, t], win[t][:, c * CH : (c + 1) * CH])
+
+        product(0)
+        gather(0)
+        smaller(0)
+        for t in range(1, PACK):
+            product(t)
+        for t in range(1, PACK):
+            gather(t)
+            scatter(t - 1)
+            for c in range(NCH):
+                if t == PACK - 1 and c < VCH:
+                    pair = win[t - 1][:, c * CH : (c + 1) * CH].rearrange("p (c o) -> p c o", o=1)
+                    nc.scalar.copy(grouped[c][:, :, t - 1 : t + 1], pair.to_broadcast([P, CH, 2]))
+                else:
+                    regroup(t - 1, c, nc.scalar.copy)
+            smaller(t)
+        scatter(PACK - 1)
+
+        words = [sb.tile([P, 2 * CH], U32, name="words%d" % c, align_bytes=64) for c in range(NCH // 2)]
+        scales = sb.tile([P, U], U8, name="scales", align_bytes=64)
+        words_out = out_1[0].rearrange("p c r -> p (c r)").bitcast(I32)
+        scales_out = out_2[0].bitcast(I32)
+
+        def quantise(c):
+            nc.vector.quantize_mx(
+                words[c // 2][:, (c % 2) * CH : (c % 2 + 1) * CH].bitcast(FP8X4),
+                scales[:, c * CH : (c + 1) * CH],
+                grouped[c][:].rearrange("p c t -> p (c t)"),
+            )
+
+        for c in range(VCH, NCH):
+            regroup(PACK - 1, c, nc.scalar.copy)
+        for c in range(VCH):
+            regroup(PACK - 1, c, nc.vector.tensor_copy)
+        for c in range(NCH):
+            quantise(c)
+            if c % 2 == 1:
+                h = c // 2
+                nc.sync.dma_start(words_out[:, h * 2 * CH : (h + 1) * 2 * CH], words[h][:].bitcast(I32))
+        for q in range(4):
+            queue = nc.scalar if q % 2 == 0 else nc.sync
+            queue.dma_start(scales_out[4 * q : 4 * q + 4, :], scales[32 * q : 32 * q + 4, :].bitcast(I32))

@@ -16,9 +16,8 @@ MIN = mybir.AluOpType.min
 
 P = 128
 PACK = 4
-CH = 256
-NCH = U // CH
-VCH = 2
+HALF = U // 2
+QUARTER = U // 4
 
 
 def tile_picked_idxput_min_lo_kernel(tc, xT, mem, w1, offs, slot, out_0, out_1, out_2):
@@ -35,50 +34,51 @@ def tile_picked_idxput_min_lo_kernel(tc, xT, mem, w1, offs, slot, out_0, out_1, 
         out_rows = out_0.rearrange("(p t) c -> p t c", t=PACK)
 
         x = [sb.tile([P, T], F32, name="x%d" % j) for j in range(PACK)]
-        w = [sb.tile([P, PACK, N // 2], F32, name="w%d" % h) for h in range(2)]
+        w = sb.tile([P, PACK, N], F32, name="w")
         win = [sb.tile([P, U], F32, name="win%d" % t) for t in range(PACK)]
 
+        nc.sync.dma_start(x[0][:], x_rows[:, 0, :])
         nc.sync.dma_start(offs_t[:], offs)
-        for j in range(PACK):
+        for j in range(1, PACK):
             nc.sync.dma_start(x[j][:], x_rows[:, j, :])
-        for h in range(2):
-            nc.sync.dma_start(w[h][:], w_rows[:, :, h * (N // 2) : (h + 1) * (N // 2)])
         nc.sync.dma_start(slot_t[:], slot)
-        for t in range(PACK):
+        for t in range(2):
+            nc.sync.dma_start(win[t][:], mem_rows[:, t, :])
+        nc.sync.dma_start(w[:], w_rows)
+        for t in range(2, PACK):
             nc.sync.dma_start(win[t][:], mem_rows[:, t, :])
 
-        xg = sb.tile([P, PACK, S], BF16, name="xg", align_bytes=64)
-        for j in range(PACK):
-            nc.vector.tensor_copy(xg[:, j, :], x[j][:].indirect(offs_t[:]))
+        xg = [sb.tile([P, 2, S], BF16, name="xg%d" % h, align_bytes=64) for h in range(2)]
         xi = sb.tile([P, S, PACK], BF16, name="xi", align_bytes=64)
-        nc.vector.tensor_copy(
-            xi[:].rearrange("p (c i) j -> p c j i", i=4), xg[:].rearrange("p j (c i) -> p c j i", i=4)
-        )
+        for h in range(2):
+            for e in range(2):
+                nc.vector.tensor_copy(xg[h][:, e, :], x[2 * h + e][:].indirect(offs_t[:]))
+            nc.scalar.copy(xi[:, :, 2 * h : 2 * h + 2], xg[h][:].rearrange("p e c -> p c e"))
         x_codes = sb.tile([P, S], U32, name="x_codes", align_bytes=64)
         x_scales = sb.tile([P, S], U8, name="x_scales", align_bytes=64)
-        nc.vector.quantize_mx(x_codes[:].bitcast(FP8X4), x_scales[:], xi[:].rearrange("p c j -> p (c j)"))
 
-        w_first = sb.tile([P, P, PACK], BF16, name="w_first", align_bytes=64)
-        w_rest = sb.tile([P, PACK - 1, P, PACK], BF16, name="w_rest", align_bytes=64)
+        wg = [sb.tile([P, 2, P, PACK], BF16, name="wg%d" % h, align_bytes=64) for h in range(2)]
+        w_dealt = w[:].rearrange("p j (m t) -> p m t j", t=PACK)
         for h in range(2):
-            src = w[h][:].rearrange("p j (m t) -> p m t j", t=PACK)
-            ms = slice(h * (P // 2), (h + 1) * (P // 2))
-            nc.scalar.copy(w_first[:, ms, :], src[:, :, 0, :])
-            nc.scalar.copy(w_rest[:, :, ms, :].rearrange("p t m j -> p m t j"), src[:, :, 1:, :])
-        w_codes = [sb.tile([P, P], U32, name="w_codes%d" % t, align_bytes=64) for t in range(PACK)]
-        w_scales = [sb.tile([P, P], U8, name="w_scales%d" % t, align_bytes=64) for t in range(PACK)]
+            nc.scalar.copy(wg[h][:].rearrange("p e m j -> p m e j"), w_dealt[:, :, 2 * h : 2 * h + 2, :])
+        w_codes = [sb.tile([P, 2 * P], U32, name="w_codes%d" % h, align_bytes=64) for h in range(2)]
+        w_scales = [sb.tile([P, 2 * P], U8, name="w_scales%d" % h, align_bytes=64) for h in range(2)]
         y = [ps.tile([P, S], F32, name="y%d" % t) for t in range(PACK)]
         old = [sb.tile([P, S], F32, name="old%d" % t) for t in range(PACK)]
         new = [sb.tile([P, S], F32, name="new%d" % t) for t in range(PACK)]
-        grouped = [sb.tile([P, CH, PACK], BF16, name="grouped%d" % c, align_bytes=64) for c in range(NCH)]
+        left = sb.tile([P, HALF, PACK], BF16, name="left", align_bytes=64)
+        right = sb.tile([P, HALF, PACK], BF16, name="right", align_bytes=64)
 
-        def product(t):
-            src = w_first[:] if t == 0 else w_rest[:, t - 1, :, :]
-            nc.vector.quantize_mx(w_codes[t][:].bitcast(FP8X4), w_scales[t][:], src.rearrange("p m j -> p (m j)"))
-            nc.tensor.matmul_mx(
-                y[t][:], w_codes[t][:].bitcast(FP8X4), w_scales[t][:], x_codes[:].bitcast(FP8X4), x_scales[:],
-                start=True, stop=True,
+        def products(h):
+            nc.vector.quantize_mx(
+                w_codes[h][:].bitcast(FP8X4), w_scales[h][:], wg[h][:].rearrange("p e m j -> p (e m j)")
             )
+            for e in range(2):
+                cols = slice(e * P, (e + 1) * P)
+                nc.tensor.matmul_mx(
+                    y[2 * h + e][:], w_codes[h][:, cols].bitcast(FP8X4), w_scales[h][:, cols],
+                    x_codes[:].bitcast(FP8X4), x_scales[:], start=True, stop=True,
+                )
 
         def gather(t):
             nc.vector.tensor_copy(old[t][:], win[t][:].indirect(slot_t[:]))
@@ -89,48 +89,46 @@ def tile_picked_idxput_min_lo_kernel(tc, xT, mem, w1, offs, slot, out_0, out_1, 
         def scatter(t):
             nc.vector.tensor_copy(win[t][:].indirect(slot_t[:]), new[t][:])
             nc.sync.dma_start(out_rows[:, t, :], win[t][:])
+            if t < 2:
+                nc.scalar.copy(left[:, :, t], win[t][:, :HALF])
+            if t == 2:
+                pair = win[t][:, :HALF].rearrange("p (c o) -> p c o", o=1)
+                nc.scalar.copy(left[:, :, 2:4], pair.to_broadcast([P, HALF, 2]))
+            if t < 3:
+                nc.scalar.copy(right[:, :, t], win[t][:, HALF:])
 
-        def regroup(t, c, engine_copy):
-            engine_copy(grouped[c][:, :, t], win[t][:, c * CH : (c + 1) * CH])
-
-        product(0)
         gather(0)
+        gather(1)
+        nc.vector.quantize_mx(x_codes[:].bitcast(FP8X4), x_scales[:], xi[:].rearrange("p c j -> p (c j)"))
+        gather(2)
+        products(0)
+        gather(3)
+        products(1)
         smaller(0)
         for t in range(1, PACK):
-            product(t)
-        for t in range(1, PACK):
-            gather(t)
-            scatter(t - 1)
-            for c in range(NCH):
-                if t == PACK - 1 and c < VCH:
-                    pair = win[t - 1][:, c * CH : (c + 1) * CH].rearrange("p (c o) -> p c o", o=1)
-                    nc.scalar.copy(grouped[c][:, :, t - 1 : t + 1], pair.to_broadcast([P, CH, 2]))
-                else:
-                    regroup(t - 1, c, nc.scalar.copy)
             smaller(t)
+            scatter(t - 1)
         scatter(PACK - 1)
 
-        words = [sb.tile([P, 2 * CH], U32, name="words%d" % c, align_bytes=64) for c in range(NCH // 2)]
         scales = sb.tile([P, U], U8, name="scales", align_bytes=64)
         words_out = out_1[0].rearrange("p c r -> p (c r)").bitcast(I32)
         scales_out = out_2[0].bitcast(I32)
 
-        def quantise(c):
+        def quantise(src, first, width):
+            words = sb.tile([P, width], U32, name="words%d" % first, align_bytes=64)
             nc.vector.quantize_mx(
-                words[c // 2][:, (c % 2) * CH : (c % 2 + 1) * CH].bitcast(FP8X4),
-                scales[:, c * CH : (c + 1) * CH],
-                grouped[c][:].rearrange("p c t -> p (c t)"),
+                words[:].bitcast(FP8X4), scales[:, first : first + width], src.rearrange("p c t -> p (c t)")
             )
+            nc.sync.dma_start(words_out[:, first : first + width], words[:].bitcast(I32))
 
-        for c in range(VCH, NCH):
-            regroup(PACK - 1, c, nc.scalar.copy)
-        for c in range(VCH):
-            regroup(PACK - 1, c, nc.vector.tensor_copy)
-        for c in range(NCH):
-            quantise(c)
-            if c % 2 == 1:
-                h = c // 2
-                nc.sync.dma_start(words_out[:, h * 2 * CH : (h + 1) * 2 * CH], words[h][:].bitcast(I32))
+        for c in range(2):
+            nc.scalar.copy(
+                right[:, c * QUARTER : (c + 1) * QUARTER, 3], win[3][:, HALF + c * QUARTER : HALF + (c + 1) * QUARTER]
+            )
+        nc.vector.tensor_copy(left[:, :, 3], win[3][:, :HALF])
+        quantise(right[:, :QUARTER, :], HALF, QUARTER)
+        quantise(left[:], 0, HALF)
+        quantise(right[:, QUARTER:, :], HALF + QUARTER, QUARTER)
         for q in range(4):
             queue = nc.scalar if q % 2 == 0 else nc.sync
             queue.dma_start(scales_out[4 * q : 4 * q + 4, :], scales[32 * q : 32 * q + 4, :].bitcast(I32))

@@ -58,9 +58,9 @@ def tile_picked_idxput_min_lo_kernel(tc, xT, mem, w1, offs, slot, out_0, out_1, 
         x_scales = sb.tile([P, S], U8, name="x_scales", align_bytes=64)
 
         wg = [sb.tile([P, 2, P, PACK], BF16, name="wg%d" % h, align_bytes=64) for h in range(2)]
-        w_dealt = w[:].rearrange("p j (m t) -> p m t j", t=PACK)
+        w_dealt = w[:].rearrange("p j (m t) -> p m j t", t=PACK)
         for h in range(2):
-            nc.scalar.copy(wg[h][:].rearrange("p e m j -> p m e j"), w_dealt[:, :, 2 * h : 2 * h + 2, :])
+            nc.scalar.copy(wg[h][:].rearrange("p e m j -> p m j e"), w_dealt[:, :, :, 2 * h : 2 * h + 2])
         w_codes = [sb.tile([P, 2 * P], U32, name="w_codes%d" % h, align_bytes=64) for h in range(2)]
         w_scales = [sb.tile([P, 2 * P], U8, name="w_scales%d" % h, align_bytes=64) for h in range(2)]
         y = [ps.tile([P, S], F32, name="y%d" % t) for t in range(PACK)]

@@ -39,21 +39,22 @@ def tile_picked_idxput_min_lo_kernel(tc, xT, mem, w1, offs, slot, out_0, out_1, 
 
         nc.sync.dma_start(x[0][:], x_rows[:, 0, :])
         nc.sync.dma_start(offs_t[:], offs)
-        for j in range(1, PACK):
+        for j in (2, 1):
             nc.sync.dma_start(x[j][:], x_rows[:, j, :])
         nc.sync.dma_start(slot_t[:], slot)
-        for t in range(2):
-            nc.sync.dma_start(win[t][:], mem_rows[:, t, :])
+        nc.sync.dma_start(win[0][:], mem_rows[:, 0, :])
+        nc.sync.dma_start(x[3][:], x_rows[:, 3, :])
+        nc.sync.dma_start(win[1][:], mem_rows[:, 1, :])
         nc.sync.dma_start(w[:], w_rows)
         for t in range(2, PACK):
             nc.sync.dma_start(win[t][:], mem_rows[:, t, :])
 
-        xg = [sb.tile([P, 2, S], BF16, name="xg%d" % h, align_bytes=64) for h in range(2)]
+        xb = [sb.tile([P, T], BF16, name="xb%d" % j, align_bytes=64) for j in range(2)]
         xi = sb.tile([P, S, PACK], BF16, name="xi", align_bytes=64)
-        for h in range(2):
-            for e in range(2):
-                nc.vector.tensor_copy(xg[h][:, e, :], x[2 * h + e][:].indirect(offs_t[:]))
-            nc.scalar.copy(xi[:, :, 2 * h : 2 * h + 2], xg[h][:].rearrange("p e c -> p c e"))
+        for j in range(2):
+            nc.scalar.copy(xb[j][:], x[j][:])
+            nc.scalar.activation(xi[:, :, j], xb[j][:].indirect(offs_t[:]), mybir.ActivationFunctionType.Copy)
+            nc.vector.tensor_copy(xi[:, :, 2 + j], x[2 + j][:].indirect(offs_t[:]))
         x_codes = sb.tile([P, S], U32, name="x_codes", align_bytes=64)
         x_scales = sb.tile([P, S], U8, name="x_scales", align_bytes=64)
 

@@ -94,7 +94,9 @@ def tile_picked_idxput_min_lo_kernel(tc, xT, mem, w1, offs, slot, out_0, out_1, 
                 nc.scalar.copy(left[:, :, t], win[t][:, :HALF])
             if t == 2:
                 pair = win[t][:, :HALF].rearrange("p (c o) -> p c o", o=1)
-                nc.scalar.copy(left[:, :, 2:4], pair.to_broadcast([P, HALF, 2]))
+                nc.gpsimd.tensor_scalar(
+                    left[:, :, 2:4], pair.to_broadcast([P, HALF, 2]), 1.0, -0.0, mybir.AluOpType.mult, mybir.AluOpType.add
+                )
             if t < 3:
                 nc.scalar.copy(right[:, :, t], win[t][:, HALF:])
 

@@ -24,6 +24,7 @@ def tile_picked_idxput_min_lo_kernel(tc, xT, mem, w1, offs, slot, out_0, out_1, 
     nc = tc.nc
     with ExitStack() as ctx:
         sb = ctx.enter_context(tc.tile_pool(name="sb", bufs=1))
+        turn = ctx.enter_context(tc.tile_pool(name="turn", bufs=1))
         ps = ctx.enter_context(tc.psum_pool(name="ps", bufs=1))
 
         offs_t = sb.tile([P, S // 16], U16, name="offs_t")
@@ -65,10 +66,18 @@ def tile_picked_idxput_min_lo_kernel(tc, xT, mem, w1, offs, slot, out_0, out_1, 
         w_codes = [sb.tile([P, 2 * P], U32, name="w_codes%d" % h, align_bytes=64) for h in range(2)]
         w_scales = [sb.tile([P, 2 * P], U8, name="w_scales%d" % h, align_bytes=64) for h in range(2)]
         y = [ps.tile([P, S], F32, name="y%d" % t) for t in range(PACK)]
-        old = [sb.tile([P, S], F32, name="old%d" % t) for t in range(PACK)]
-        new = [sb.tile([P, S], F32, name="new%d" % t) for t in range(PACK)]
-        left = sb.tile([P, HALF, PACK], BF16, name="left", align_bytes=64)
-        right = sb.tile([P, HALF, PACK], BF16, name="right", align_bytes=64)
+        both = sb.tile([P, 2, S], F32, name="both")
+        old = [sb.tile([P, S], F32, name="old%d" % t)[:] for t in range(PACK - 1)] + [both[:, 0, :]]
+        new = [sb.tile([P, S], F32, name="new%d" % t, tag="new%d" % t) for t in range(PACK - 1)]
+        side = sb.tile([P, S], F32, name="side")
+        sign = turn.tile([P, S], F32, name="sign", offset=3072, align_bytes=64)
+        share = sb.tile([P, 2, S], F32, name="share")
+        parts = [sb.tile([P, 2, S // 2], F32, name="parts%d" % c) for c in range(2)]
+        halves = (slice(0, S // 2), slice(S // 2, S))
+        half = sb.tile([P, 1], F32, name="half")
+        nc.gpsimd.memset(half[:], 0.5)
+        left = turn.tile([P, HALF, PACK], BF16, name="left", offset=0, align_bytes=64)
+        right = turn.tile([P, HALF, PACK], BF16, name="right", offset=4096, align_bytes=64)
 
         def products(h):
             nc.vector.quantize_mx(
@@ -82,10 +91,10 @@ def tile_picked_idxput_min_lo_kernel(tc, xT, mem, w1, offs, slot, out_0, out_1, 
                 )
 
         def gather(t):
-            nc.vector.tensor_copy(old[t][:], win[t][:].indirect(slot_t[:]))
+            nc.vector.tensor_copy(old[t], win[t][:].indirect(slot_t[:]))
 
         def smaller(t):
-            nc.vector.tensor_tensor(new[t][:], y[t][:], old[t][:], MIN)
+            nc.vector.tensor_tensor(new[t][:], y[t][:], old[t], MIN)
 
         def scatter(t):
             nc.vector.tensor_copy(win[t][:].indirect(slot_t[:]), new[t][:])
@@ -107,11 +116,25 @@ def tile_picked_idxput_min_lo_kernel(tc, xT, mem, w1, offs, slot, out_0, out_1, 
         products(0)
         gather(3)
         products(1)
+        nc.scalar.copy(both[:, 1, :], y[3][:])
+        nc.gpsimd.tensor_tensor(side[:], both[:, 0, :], both[:, 1, :], mybir.AluOpType.subtract)
+        nc.scalar.activation(sign[:], side[:], mybir.ActivationFunctionType.Sign)
+        for i, scale in enumerate((-0.5, 0.5)):
+            nc.scalar.activation(
+                share[:, i, :], sign[:], mybir.ActivationFunctionType.Identity, bias=half[:], scale=scale
+            )
+        for c in range(2):
+            nc.gpsimd.tensor_tensor(parts[c][:], both[:, :, halves[c]], share[:, :, halves[c]], mybir.AluOpType.mult)
         smaller(0)
-        for t in range(1, PACK):
-            smaller(t)
-            scatter(t - 1)
-        scatter(PACK - 1)
+        smaller(1)
+        scatter(0)
+        smaller(2)
+        scatter(1)
+        new.append(sb.tile([P, S], F32, name="new3", tag="new1"))
+        for c in range(2):
+            nc.gpsimd.tensor_tensor(new[3][:, halves[c]], parts[c][:, 0, :], parts[c][:, 1, :], mybir.AluOpType.add)
+        scatter(2)
+        scatter(3)
 
         scales = sb.tile([P, U], U8, name="scales", align_bytes=64)
         words_out = out_1[0].rearrange("p c r -> p (c r)").bitcast(I32)

@@ -66,13 +66,13 @@ def tile_picked_idxput_min_lo_kernel(tc, xT, mem, w1, offs, slot, out_0, out_1, 
         w_codes = [sb.tile([P, 2 * P], U32, name="w_codes%d" % h, align_bytes=64) for h in range(2)]
         w_scales = [sb.tile([P, 2 * P], U8, name="w_scales%d" % h, align_bytes=64) for h in range(2)]
         y = [ps.tile([P, S], F32, name="y%d" % t) for t in range(PACK)]
-        both = sb.tile([P, 2, S], F32, name="both")
-        old = [sb.tile([P, S], F32, name="old%d" % t)[:] for t in range(PACK - 1)] + [both[:, 0, :]]
+        both = [sb.tile([P, 2, S], F32, name="both%d" % e) for e in range(2)]
+        old = [sb.tile([P, S], F32, name="old%d" % t)[:] for t in range(2)] + [both[e][:, 0, :] for e in range(2)]
         new = [sb.tile([P, S], F32, name="new%d" % t, tag="new%d" % t) for t in range(PACK - 1)]
-        side = sb.tile([P, S], F32, name="side")
+        side = [sb.tile([P, S], F32, name="side%d" % e) for e in range(2)]
         sign = turn.tile([P, S], F32, name="sign", offset=3072, align_bytes=64)
-        share = sb.tile([P, 2, S], F32, name="share")
-        parts = [sb.tile([P, 2, S // 2], F32, name="parts%d" % c) for c in range(2)]
+        share = [sb.tile([P, 2, S], F32, name="share%d" % e) for e in range(2)]
+        parts = sb.tile([P, 2, S], F32, name="parts")
         halves = (slice(0, S // 2), slice(S // 2, S))
         half = sb.tile([P, 1], F32, name="half")
         nc.gpsimd.memset(half[:], 0.5)
@@ -109,6 +109,24 @@ def tile_picked_idxput_min_lo_kernel(tc, xT, mem, w1, offs, slot, out_0, out_1, 
             if t < 3:
                 nc.scalar.copy(right[:, :, t], win[t][:, HALF:])
 
+        def compare(e, cols):
+            nc.scalar.copy(both[e][:, 1, cols], y[2 + e][:, cols])
+            nc.gpsimd.tensor_tensor(side[e][:, cols], both[e][:, 0, cols], both[e][:, 1, cols], mybir.AluOpType.subtract)
+
+        def masks(e, cols):
+            nc.scalar.activation(sign[:, cols], side[e][:, cols], mybir.ActivationFunctionType.Sign)
+            for i, scale in enumerate((-0.5, 0.5)):
+                nc.scalar.activation(
+                    share[e][:, i, cols], sign[:, cols], mybir.ActivationFunctionType.Identity, bias=half[:], scale=scale
+                )
+
+        def weigh(e, cols, room):
+            nc.gpsimd.tensor_tensor(parts[:, :, room], both[e][:, :, cols], share[e][:, :, cols], mybir.AluOpType.mult)
+
+        def join(e, cols, room):
+            nc.gpsimd.tensor_tensor(new[2 + e][:, cols], parts[:, 0, room], parts[:, 1, room], mybir.AluOpType.add)
+
+        middle = slice(S // 4, 3 * S // 4)
         gather(0)
         gather(1)
         nc.vector.quantize_mx(x_codes[:].bitcast(FP8X4), x_scales[:], xi[:].rearrange("p c j -> p (c j)"))
@@ -116,23 +134,22 @@ def tile_picked_idxput_min_lo_kernel(tc, xT, mem, w1, offs, slot, out_0, out_1, 
         products(0)
         gather(3)
         products(1)
-        nc.scalar.copy(both[:, 1, :], y[3][:])
-        nc.gpsimd.tensor_tensor(side[:], both[:, 0, :], both[:, 1, :], mybir.AluOpType.subtract)
-        nc.scalar.activation(sign[:], side[:], mybir.ActivationFunctionType.Sign)
-        for i, scale in enumerate((-0.5, 0.5)):
-            nc.scalar.activation(
-                share[:, i, :], sign[:], mybir.ActivationFunctionType.Identity, bias=half[:], scale=scale
-            )
+        compare(0, halves[0])
+        compare(1, slice(0, S))
+        masks(0, halves[0])
+        masks(1, slice(0, S))
+        weigh(0, halves[0], middle)
+        join(0, halves[0], middle)
         for c in range(2):
-            nc.gpsimd.tensor_tensor(parts[c][:], both[:, :, halves[c]], share[:, :, halves[c]], mybir.AluOpType.mult)
+            weigh(1, halves[c], halves[c])
         smaller(0)
         smaller(1)
         scatter(0)
-        smaller(2)
+        nc.vector.tensor_tensor(new[2][:, halves[1]], y[2][:, halves[1]], old[2][:, halves[1]], MIN)
         scatter(1)
         new.append(sb.tile([P, S], F32, name="new3", tag="new1"))
         for c in range(2):
-            nc.gpsimd.tensor_tensor(new[3][:, halves[c]], parts[c][:, 0, :], parts[c][:, 1, :], mybir.AluOpType.add)
+            join(1, halves[c], halves[c])
         scatter(2)
         scatter(3)
 

@@ -13,22 +13,23 @@ U16 = mybir.dt.uint16
 U8 = mybir.dt.uint8
 FP8X4 = mybir.dt.float8_e4m3fn_x4
 MIN = mybir.AluOpType.min
+COPY = mybir.ActivationFunctionType.Copy
 
 P = 128
 PACK = 4
 HALF = U // 2
-QUARTER = U // 4
+H = S // 2
+GROUP = 16
 
 
 def tile_picked_idxput_min_lo_kernel(tc, xT, mem, w1, offs, slot, out_0, out_1, out_2):
     nc = tc.nc
     with ExitStack() as ctx:
         sb = ctx.enter_context(tc.tile_pool(name="sb", bufs=1))
-        turn = ctx.enter_context(tc.tile_pool(name="turn", bufs=1))
         ps = ctx.enter_context(tc.psum_pool(name="ps", bufs=1))
 
-        offs_t = sb.tile([P, S // 16], U16, name="offs_t")
-        slot_t = sb.tile([P, S // 16], U16, name="slot_t")
+        offs_t = sb.tile([P, S // GROUP], U16, name="offs_t")
+        slot_t = sb.tile([P, S // GROUP], U16, name="slot_t")
         x_rows = xT.rearrange("(p j) c -> p j c", j=PACK)
         w_rows = w1.rearrange("(p j) c -> p j c", j=PACK)
         mem_rows = mem.rearrange("(p t) c -> p t c", t=PACK)
@@ -40,138 +41,123 @@ def tile_picked_idxput_min_lo_kernel(tc, xT, mem, w1, offs, slot, out_0, out_1, 
 
         nc.sync.dma_start(x[0][:], x_rows[:, 0, :])
         nc.sync.dma_start(offs_t[:], offs)
-        for j in (2, 1):
+        for j in range(1, PACK):
             nc.sync.dma_start(x[j][:], x_rows[:, j, :])
-        nc.sync.dma_start(slot_t[:], slot)
-        nc.sync.dma_start(win[0][:], mem_rows[:, 0, :])
-        nc.sync.dma_start(x[3][:], x_rows[:, 3, :])
-        nc.sync.dma_start(win[1][:], mem_rows[:, 1, :])
         nc.sync.dma_start(w[:], w_rows)
-        for t in range(2, PACK):
+        nc.sync.dma_start(slot_t[:], slot)
+        for t in (0, 2, 1, 3):
             nc.sync.dma_start(win[t][:], mem_rows[:, t, :])
 
-        xb = [sb.tile([P, T], BF16, name="xb%d" % j, align_bytes=64) for j in range(2)]
-        xi = sb.tile([P, S, PACK], BF16, name="xi", align_bytes=64)
-        for j in range(2):
-            nc.scalar.copy(xb[j][:], x[j][:])
-            nc.scalar.activation(xi[:, :, j], xb[j][:].indirect(offs_t[:]), mybir.ActivationFunctionType.Copy)
-            nc.vector.tensor_copy(xi[:, :, 2 + j], x[2 + j][:].indirect(offs_t[:]))
-        x_codes = sb.tile([P, S], U32, name="x_codes", align_bytes=64)
-        x_scales = sb.tile([P, S], U8, name="x_scales", align_bytes=64)
+        def entries(first, count):
+            return slice(first // GROUP, (first + count) // GROUP)
+
+        def copy_on(engine, dst, src):
+            if engine == "vector":
+                nc.vector.tensor_copy(dst, src)
+            else:
+                nc.scalar.activation(dst, src, COPY)
+
+        picked = sb.tile([P, PACK, S], BF16, name="picked", align_bytes=64)
+        x0 = sb.tile([P, T], BF16, name="x0_rounded", align_bytes=64)
+        nc.scalar.copy(x0[:, : T // 4], x[0][:, : T // 4])
+        nc.vector.tensor_copy(x0[:, T // 4 :], x[0][:, T // 4 :])
+        copy_on("scalar", picked[:, 0, :], x0[:].indirect(offs_t[:]))
+        copy_on("vector", picked[:, 1, :], x[1][:].indirect(offs_t[:]))
+        copy_on("scalar", picked[:, 2, :], x[2][:].indirect(offs_t[:]))
+        copy_on("vector", picked[:, 3, :H], x[3][:].indirect(offs_t[:, entries(0, H)]))
+        copy_on("scalar", picked[:, 3, H:], x[3][:].indirect(offs_t[:, entries(H, H)]))
+        xi = [sb.tile([P, H, PACK], BF16, name="xi%d" % h, align_bytes=64) for h in range(2)]
+        nc.vector.tensor_copy(xi[0][:], picked[:, :, :H].rearrange("p j s -> p s j"))
+        nc.scalar.copy(xi[1][:], picked[:, :, H:].rearrange("p j s -> p s j"))
+        x_codes = [sb.tile([P, H], U32, name="x_codes%d" % h, align_bytes=64) for h in range(2)]
+        x_scales = [sb.tile([P, H], U8, name="x_scales%d" % h, align_bytes=64) for h in range(2)]
+        for h in range(2):
+            nc.vector.quantize_mx(x_codes[h][:].bitcast(FP8X4), x_scales[h][:], xi[h][:].rearrange("p c j -> p (c j)"))
 
         wg = [sb.tile([P, 2, P, PACK], BF16, name="wg%d" % h, align_bytes=64) for h in range(2)]
         w_dealt = w[:].rearrange("p j (m t) -> p m j t", t=PACK)
-        for h in range(2):
-            nc.scalar.copy(wg[h][:].rearrange("p e m j -> p m j e"), w_dealt[:, :, :, 2 * h : 2 * h + 2])
+        nc.vector.tensor_copy(wg[0][:].rearrange("p e m j -> p m j e"), w_dealt[:, :, :, 0:2])
+        nc.scalar.copy(wg[1][:].rearrange("p e m j -> p m j e"), w_dealt[:, :, :, 2:4])
         w_codes = [sb.tile([P, 2 * P], U32, name="w_codes%d" % h, align_bytes=64) for h in range(2)]
         w_scales = [sb.tile([P, 2 * P], U8, name="w_scales%d" % h, align_bytes=64) for h in range(2)]
-        y = [ps.tile([P, S], F32, name="y%d" % t) for t in range(PACK)]
-        both = [sb.tile([P, 2, S], F32, name="both%d" % e) for e in range(2)]
-        old = [sb.tile([P, S], F32, name="old%d" % t)[:] for t in range(2)] + [both[e][:, 0, :] for e in range(2)]
-        new = [sb.tile([P, S], F32, name="new%d" % t, tag="new%d" % t) for t in range(PACK - 1)]
-        side = [sb.tile([P, S], F32, name="side%d" % e) for e in range(2)]
-        sign = turn.tile([P, S], F32, name="sign", offset=3072, align_bytes=64)
-        share = [sb.tile([P, 2, S], F32, name="share%d" % e) for e in range(2)]
-        parts = sb.tile([P, 2, S], F32, name="parts")
-        halves = (slice(0, S // 2), slice(S // 2, S))
-        half = sb.tile([P, 1], F32, name="half")
-        nc.gpsimd.memset(half[:], 0.5)
-        left = turn.tile([P, HALF, PACK], BF16, name="left", offset=0, align_bytes=64)
-        right = turn.tile([P, HALF, PACK], BF16, name="right", offset=4096, align_bytes=64)
-
-        def products(h):
+        for h in range(2):
             nc.vector.quantize_mx(
                 w_codes[h][:].bitcast(FP8X4), w_scales[h][:], wg[h][:].rearrange("p e m j -> p (e m j)")
             )
-            for e in range(2):
+
+        old = [sb.tile([P, 2 * S], F32, name="old%d" % h) for h in range(2)]
+        new = [sb.tile([P, 2 * S], F32, name="new%d" % h) for h in range(2)]
+        pairs = sb.tile([P, 2, U, 2], BF16, name="pairs", align_bytes=64)
+
+        def gather(engine, t, first, count):
+            at = (t % 2) * S + first
+            copy_on(engine, old[t // 2][:, at : at + count], win[t][:].indirect(slot_t[:, entries(first, count)]))
+
+        def smaller(h, at, count):
+            y = ps.tile([P, count], F32, name="y%d_%d" % (h, at))
+            for c in range(0, count, H):
+                e, first = divmod(at + c, S)
                 cols = slice(e * P, (e + 1) * P)
                 nc.tensor.matmul_mx(
-                    y[2 * h + e][:], w_codes[h][:, cols].bitcast(FP8X4), w_scales[h][:, cols],
-                    x_codes[:].bitcast(FP8X4), x_scales[:], start=True, stop=True,
+                    y[:, c : c + H], w_codes[h][:, cols].bitcast(FP8X4), w_scales[h][:, cols],
+                    x_codes[first // H][:].bitcast(FP8X4), x_scales[first // H][:], start=True, stop=True,
                 )
+            nc.vector.tensor_tensor(new[h][:, at : at + count], y[:], old[h][:, at : at + count], MIN)
 
-        def gather(t):
-            nc.vector.tensor_copy(old[t], win[t][:].indirect(slot_t[:]))
+        def scatter(engine, t, first, count):
+            at = (t % 2) * S + first
+            copy_on(engine, win[t][:].indirect(slot_t[:, entries(first, count)]), new[t // 2][:, at : at + count])
 
-        def smaller(t):
-            nc.vector.tensor_tensor(new[t][:], y[t][:], old[t], MIN)
-
-        def scatter(t):
-            nc.vector.tensor_copy(win[t][:].indirect(slot_t[:]), new[t][:])
+        def store(t):
             nc.sync.dma_start(out_rows[:, t, :], win[t][:])
-            if t < 2:
-                nc.scalar.copy(left[:, :, t], win[t][:, :HALF])
-            if t == 2:
-                pair = win[t][:, :HALF].rearrange("p (c o) -> p c o", o=1)
-                nc.gpsimd.tensor_scalar(
-                    left[:, :, 2:4], pair.to_broadcast([P, HALF, 2]), 1.0, -0.0, mybir.AluOpType.mult, mybir.AluOpType.add
-                )
-            if t < 3:
-                nc.scalar.copy(right[:, :, t], win[t][:, HALF:])
 
-        def compare(e, cols):
-            nc.scalar.copy(both[e][:, 1, cols], y[2 + e][:, cols])
-            nc.gpsimd.tensor_tensor(side[e][:, cols], both[e][:, 0, cols], both[e][:, 1, cols], mybir.AluOpType.subtract)
+        def round_early(t):
+            nc.gpsimd.tensor_scalar(pairs[:, 0, :, t], win[t][:], 1.0, -0.0, mybir.AluOpType.mult, mybir.AluOpType.add)
 
-        def masks(e, cols):
-            nc.scalar.activation(sign[:, cols], side[e][:, cols], mybir.ActivationFunctionType.Sign)
-            for i, scale in enumerate((-0.5, 0.5)):
-                nc.scalar.activation(
-                    share[e][:, i, cols], sign[:, cols], mybir.ActivationFunctionType.Identity, bias=half[:], scale=scale
-                )
-
-        def weigh(e, cols, room):
-            nc.gpsimd.tensor_tensor(parts[:, :, room], both[e][:, :, cols], share[e][:, :, cols], mybir.AluOpType.mult)
-
-        def join(e, cols, room):
-            nc.gpsimd.tensor_tensor(new[2 + e][:, cols], parts[:, 0, room], parts[:, 1, room], mybir.AluOpType.add)
-
-        middle = slice(S // 4, 3 * S // 4)
-        gather(0)
-        gather(1)
-        nc.vector.quantize_mx(x_codes[:].bitcast(FP8X4), x_scales[:], xi[:].rearrange("p c j -> p (c j)"))
-        gather(2)
-        products(0)
-        gather(3)
-        products(1)
-        compare(0, halves[0])
-        compare(1, slice(0, S))
-        masks(0, halves[0])
-        masks(1, slice(0, S))
-        weigh(0, halves[0], middle)
-        join(0, halves[0], middle)
-        for c in range(2):
-            weigh(1, halves[c], halves[c])
-        smaller(0)
-        smaller(1)
-        scatter(0)
-        nc.vector.tensor_tensor(new[2][:, halves[1]], y[2][:, halves[1]], old[2][:, halves[1]], MIN)
-        scatter(1)
-        new.append(sb.tile([P, S], F32, name="new3", tag="new1"))
-        for c in range(2):
-            join(1, halves[c], halves[c])
-        scatter(2)
-        scatter(3)
+        gather("scalar", 0, 0, H)
+        gather("scalar", 0, H, H)
+        smaller(0, 0, H)
+        gather("scalar", 2, 0, H)
+        gather("vector", 2, H, H)
+        scatter("vector", 0, 0, H)
+        gather("scalar", 1, 0, S)
+        smaller(1, 0, H)
+        smaller(0, H, S)
+        gather("scalar", 3, 0, S)
+        smaller(0, S + H, H)
+        scatter("scalar", 1, 0, H)
+        scatter("vector", 0, H, H)
+        store(0)
+        round_early(0)
+        smaller(1, S + H, H)
+        smaller(1, H, S)
+        scatter("scalar", 1, H, H)
+        store(1)
+        round_early(1)
+        scatter("vector", 2, 0, S)
+        store(2)
+        scatter("scalar", 3, 0, H)
+        scatter("scalar", 3, H, H)
+        store(3)
+        nc.vector.tensor_copy(pairs[:, 1, :, 0], win[2][:])
 
         scales = sb.tile([P, U], U8, name="scales", align_bytes=64)
         words_out = out_1[0].rearrange("p c r -> p (c r)").bitcast(I32)
         scales_out = out_2[0].bitcast(I32)
-
-        def quantise(src, first, width):
-            words = sb.tile([P, width], U32, name="words%d" % first, align_bytes=64)
-            nc.vector.quantize_mx(
-                words[:].bitcast(FP8X4), scales[:, first : first + width], src.rearrange("p c t -> p (c t)")
-            )
-            nc.sync.dma_start(words_out[:, first : first + width], words[:].bitcast(I32))
-
+        pair_words = pairs[:].rearrange("p u c e -> p u (c e)").bitcast(U32)
+        pair_ints = pairs[:].rearrange("p u c e -> p u (c e)").bitcast(I32)
+        woven = [sb.tile([P, HALF, 2], U32, name="woven%d" % c, align_bytes=64) for c in range(2)]
+        sides = (slice(0, HALF), slice(HALF, U))
+        for c in (1, 0):
+            nc.vector.tensor_copy(pairs[:, 1, sides[c], 1], win[3][:, sides[c]])
+        nc.scalar.copy(woven[1][:], pair_words[:, :, sides[1]].rearrange("p u c -> p c u"))
+        nc.vector.tensor_copy(woven[0][:].bitcast(I32), pair_ints[:, :, sides[0]].rearrange("p u c -> p c u"))
         for c in range(2):
-            nc.scalar.copy(
-                right[:, c * QUARTER : (c + 1) * QUARTER, 3], win[3][:, HALF + c * QUARTER : HALF + (c + 1) * QUARTER]
+            words = sb.tile([P, HALF], U32, name="words%d" % c, align_bytes=64)
+            nc.vector.quantize_mx(
+                words[:].bitcast(FP8X4), scales[:, sides[c]], woven[c][:].rearrange("p c u -> p (c u)").bitcast(BF16)
             )
-        nc.vector.tensor_copy(left[:, :, 3], win[3][:, :HALF])
-        quantise(right[:, :QUARTER, :], HALF, QUARTER)
-        quantise(left[:], 0, HALF)
-        quantise(right[:, QUARTER:, :], HALF + QUARTER, QUARTER)
+            nc.sync.dma_start(words_out[:, sides[c]], words[:].bitcast(I32))
         for q in range(4):
             queue = nc.scalar if q % 2 == 0 else nc.sync
             queue.dma_start(scales_out[4 * q : 4 * q + 4, :], scales[32 * q : 32 * q + 4, :].bitcast(I32))

@@ -18,8 +18,10 @@ COPY = mybir.ActivationFunctionType.Copy
 P = 128
 PACK = 4
 HALF = U // 2
+JOIN = 640
 H = S // 2
 GROUP = 16
+WEAVE = 96
 
 
 def tile_picked_idxput_min_lo_kernel(tc, xT, mem, w1, offs, slot, out_0, out_1, out_2):
@@ -45,7 +47,7 @@ def tile_picked_idxput_min_lo_kernel(tc, xT, mem, w1, offs, slot, out_0, out_1, 
             nc.sync.dma_start(x[j][:], x_rows[:, j, :])
         nc.sync.dma_start(w[:], w_rows)
         nc.sync.dma_start(slot_t[:], slot)
-        for t in (0, 2, 1, 3):
+        for t in (0, 1, 3, 2):
             nc.sync.dma_start(win[t][:], mem_rows[:, t, :])
 
         def entries(first, count):
@@ -57,56 +59,67 @@ def tile_picked_idxput_min_lo_kernel(tc, xT, mem, w1, offs, slot, out_0, out_1, 
             else:
                 nc.scalar.activation(dst, src, COPY)
 
-        picked = sb.tile([P, PACK, S], BF16, name="picked", align_bytes=64)
+        picked = [sb.tile([P, PACK, H], BF16, name="picked%d" % h, align_bytes=64) for h in range(2)]
         x0 = sb.tile([P, T], BF16, name="x0_rounded", align_bytes=64)
         nc.scalar.copy(x0[:, : T // 4], x[0][:, : T // 4])
         nc.vector.tensor_copy(x0[:, T // 4 :], x[0][:, T // 4 :])
-        copy_on("scalar", picked[:, 0, :], x0[:].indirect(offs_t[:]))
-        copy_on("vector", picked[:, 1, :], x[1][:].indirect(offs_t[:]))
-        copy_on("scalar", picked[:, 2, :], x[2][:].indirect(offs_t[:]))
-        copy_on("vector", picked[:, 3, :H], x[3][:].indirect(offs_t[:, entries(0, H)]))
-        copy_on("scalar", picked[:, 3, H:], x[3][:].indirect(offs_t[:, entries(H, H)]))
-        xi = [sb.tile([P, H, PACK], BF16, name="xi%d" % h, align_bytes=64) for h in range(2)]
-        nc.vector.tensor_copy(xi[0][:], picked[:, :, :H].rearrange("p j s -> p s j"))
-        nc.scalar.copy(xi[1][:], picked[:, :, H:].rearrange("p j s -> p s j"))
-        x_codes = [sb.tile([P, H], U32, name="x_codes%d" % h, align_bytes=64) for h in range(2)]
-        x_scales = [sb.tile([P, H], U8, name="x_scales%d" % h, align_bytes=64) for h in range(2)]
-        for h in range(2):
-            nc.vector.quantize_mx(x_codes[h][:].bitcast(FP8X4), x_scales[h][:], xi[h][:].rearrange("p c j -> p (c j)"))
+        for j, window in enumerate([x0] + x[1:]):
+            for h, engine in enumerate(("vector", "scalar")):
+                copy_on(engine, picked[h][:, j, :], window[:].indirect(offs_t[:, entries(h * H, H)]))
+        early = sb.tile([P, H, PACK], BF16, name="early", align_bytes=64)
+        late = sb.tile([P, 2, H, PACK], BF16, name="late", align_bytes=64)
+        nc.vector.tensor_copy(early[:], picked[0][:].rearrange("p j s -> p s j"))
+        nc.vector.tensor_copy(late[:, 0, :WEAVE, :], picked[1][:, :, :WEAVE].rearrange("p j s -> p s j"))
+        nc.scalar.copy(late[:, 0, WEAVE:, :], picked[1][:, :, WEAVE:].rearrange("p j s -> p s j"))
+        codes = sb.tile([P, S + 2 * P], U32, name="codes", align_bytes=64)
+        exps = sb.tile([P, S + 2 * P], U8, name="exps", align_bytes=64)
+        nc.vector.quantize_mx(codes[:, :H].bitcast(FP8X4), exps[:, :H], early[:].rearrange("p c j -> p (c j)"))
 
-        wg = [sb.tile([P, 2, P, PACK], BF16, name="wg%d" % h, align_bytes=64) for h in range(2)]
+        wg = sb.tile([P, 2, P, PACK], BF16, name="wg", align_bytes=64)
         w_dealt = w[:].rearrange("p j (m t) -> p m j t", t=PACK)
-        nc.vector.tensor_copy(wg[0][:].rearrange("p e m j -> p m j e"), w_dealt[:, :, :, 0:2])
-        nc.scalar.copy(wg[1][:].rearrange("p e m j -> p m j e"), w_dealt[:, :, :, 2:4])
-        w_codes = [sb.tile([P, 2 * P], U32, name="w_codes%d" % h, align_bytes=64) for h in range(2)]
-        w_scales = [sb.tile([P, 2 * P], U8, name="w_scales%d" % h, align_bytes=64) for h in range(2)]
-        for h in range(2):
-            nc.vector.quantize_mx(
-                w_codes[h][:].bitcast(FP8X4), w_scales[h][:], wg[h][:].rearrange("p e m j -> p (e m j)")
-            )
+        nc.vector.tensor_copy(wg[:].rearrange("p e m j -> p m j e"), w_dealt[:, :, :, 0:2])
+        nc.scalar.copy(late[:, 1].rearrange("p (e m) j -> p m j e", e=2), w_dealt[:, :, :, 2:4])
+        first_codes = sb.tile([P, 2 * P], U32, name="first_codes", align_bytes=64)
+        first_exps = sb.tile([P, 2 * P], U8, name="first_exps", align_bytes=64)
+        nc.vector.quantize_mx(first_codes[:].bitcast(FP8X4), first_exps[:], wg[:].rearrange("p e m j -> p (e m j)"))
+        nc.vector.quantize_mx(codes[:, H:].bitcast(FP8X4), exps[:, H:], late[:].rearrange("p a c j -> p (a c j)"))
+        x_codes, x_scales = codes[:, :S], exps[:, :S]
+        w_codes, w_scales = [first_codes[:], codes[:, S:]], [first_exps[:], exps[:, S:]]
 
-        old = [sb.tile([P, 2 * S], F32, name="old%d" % h) for h in range(2)]
-        new = [sb.tile([P, 2 * S], F32, name="new%d" % h) for h in range(2)]
+        old_tiles = [sb.tile([P, n * H], F32, name="old%d" % i) for i, n in enumerate((1, 1, 2, 4))]
+        new_tiles = [sb.tile([P, n * H], F32, name="new%d" % i) for i, n in enumerate((1, 1, 2, 3, 1))]
+        place = {(0, 0): (0, 0), (0, 1): (1, 0), (1, 0): (2, 0), (1, 1): (2, H), (2, 0): (3, 0), (2, 1): (3, H), (3, 0): (3, S)}
+
+        def old(t, first, count):
+            i, at = place.get((t, first // H), (3, S + H))
+            return old_tiles[i][:, at : at + count]
+
+        def new(t, first, count):
+            i, at = place.get((t, first // H), (4, 0))
+            return new_tiles[i][:, at : at + count]
+
         pairs = sb.tile([P, 2, U, 2], BF16, name="pairs", align_bytes=64)
 
         def gather(engine, t, first, count):
-            at = (t % 2) * S + first
-            copy_on(engine, old[t // 2][:, at : at + count], win[t][:].indirect(slot_t[:, entries(first, count)]))
+            copy_on(engine, old(t, first, count), win[t][:].indirect(slot_t[:, entries(first, count)]))
 
-        def smaller(h, at, count):
-            y = ps.tile([P, count], F32, name="y%d_%d" % (h, at))
-            for c in range(0, count, H):
-                e, first = divmod(at + c, S)
-                cols = slice(e * P, (e + 1) * P)
+        def smaller(*pieces):
+            t0, first0, count0 = pieces[0]
+            total = sum(piece[2] for piece in pieces)
+            y = ps.tile([P, total], F32, name="y%d_%d" % (t0, first0))
+            done = 0
+            for t, first, count in pieces:
+                rows = slice((t % 2) * P, (t % 2 + 1) * P)
+                cols = slice(first, first + count)
                 nc.tensor.matmul_mx(
-                    y[:, c : c + H], w_codes[h][:, cols].bitcast(FP8X4), w_scales[h][:, cols],
-                    x_codes[first // H][:].bitcast(FP8X4), x_scales[first // H][:], start=True, stop=True,
+                    y[:, done : done + count], w_codes[t // 2][:, rows].bitcast(FP8X4), w_scales[t // 2][:, rows],
+                    x_codes[:, cols].bitcast(FP8X4), x_scales[:, cols], start=True, stop=True,
                 )
-            nc.vector.tensor_tensor(new[h][:, at : at + count], y[:], old[h][:, at : at + count], MIN)
+                done = done + count
+            nc.vector.tensor_tensor(new(t0, first0, total), y[:], old(t0, first0, total), MIN)
 
         def scatter(engine, t, first, count):
-            at = (t % 2) * S + first
-            copy_on(engine, win[t][:].indirect(slot_t[:, entries(first, count)]), new[t // 2][:, at : at + count])
+            copy_on(engine, win[t][:].indirect(slot_t[:, entries(first, count)]), new(t, first, count))
 
         def store(t):
             nc.sync.dma_start(out_rows[:, t, :], win[t][:])
@@ -116,30 +129,27 @@ def tile_picked_idxput_min_lo_kernel(tc, xT, mem, w1, offs, slot, out_0, out_1, 
 
         gather("scalar", 0, 0, H)
         gather("scalar", 0, H, H)
-        smaller(0, 0, H)
-        gather("scalar", 2, 0, H)
-        gather("vector", 2, H, H)
-        scatter("vector", 0, 0, H)
-        gather("scalar", 1, 0, S)
-        smaller(1, 0, H)
-        smaller(0, H, S)
-        gather("scalar", 3, 0, S)
-        smaller(0, S + H, H)
-        scatter("scalar", 1, 0, H)
-        scatter("vector", 0, H, H)
+        for first in (0, H):
+            smaller((0, first, H))
+            scatter("scalar", 0, first, H)
         store(0)
         round_early(0)
-        smaller(1, S + H, H)
-        smaller(1, H, S)
-        scatter("scalar", 1, H, H)
+        gather("vector", 1, 0, S)
+        smaller((1, 0, S))
+        gather("vector", 3, 0, S)
+        gather("vector", 2, 0, S)
+        smaller((3, H, H))
+        smaller((2, 0, H))
+        smaller((2, H, H), (3, 0, H))
+        for first in (0, H):
+            scatter("scalar", 1, first, H)
         store(1)
         round_early(1)
         scatter("vector", 2, 0, S)
         store(2)
-        scatter("scalar", 3, 0, H)
-        scatter("scalar", 3, H, H)
+        for first in (H, 0):
+            scatter("scalar", 3, first, H)
         store(3)
-        nc.vector.tensor_copy(pairs[:, 1, :, 0], win[2][:])
 
         scales = sb.tile([P, U], U8, name="scales", align_bytes=64)
         words_out = out_1[0].rearrange("p c r -> p (c r)").bitcast(I32)
@@ -147,17 +157,22 @@ def tile_picked_idxput_min_lo_kernel(tc, xT, mem, w1, offs, slot, out_0, out_1, 
         pair_words = pairs[:].rearrange("p u c e -> p u (c e)").bitcast(U32)
         pair_ints = pairs[:].rearrange("p u c e -> p u (c e)").bitcast(I32)
         woven = [sb.tile([P, HALF, 2], U32, name="woven%d" % c, align_bytes=64) for c in range(2)]
-        sides = (slice(0, HALF), slice(HALF, U))
-        for c in (1, 0):
-            nc.vector.tensor_copy(pairs[:, 1, sides[c], 1], win[3][:, sides[c]])
-        nc.scalar.copy(woven[1][:], pair_words[:, :, sides[1]].rearrange("p u c -> p c u"))
-        nc.vector.tensor_copy(woven[0][:].bitcast(I32), pair_ints[:, :, sides[0]].rearrange("p u c -> p c u"))
+        for t in (3, 2):
+            nc.scalar.copy(pairs[:, 1, JOIN:, t % 2], win[t][:, JOIN:])
+        for t in (2, 3):
+            nc.vector.tensor_copy(pairs[:, 1, :JOIN, t % 2], win[t][:, :JOIN])
+        nc.scalar.copy(woven[1][:, JOIN - HALF :, :], pair_words[:, :, JOIN:].rearrange("p u c -> p c u"))
+        nc.vector.tensor_copy(woven[0][:].bitcast(I32), pair_ints[:, :, :HALF].rearrange("p u c -> p c u"))
+        nc.vector.tensor_copy(
+            woven[1][:, : JOIN - HALF, :].bitcast(I32), pair_ints[:, :, HALF:JOIN].rearrange("p u c -> p c u")
+        )
         for c in range(2):
+            cols = slice(c * HALF, (c + 1) * HALF)
             words = sb.tile([P, HALF], U32, name="words%d" % c, align_bytes=64)
             nc.vector.quantize_mx(
-                words[:].bitcast(FP8X4), scales[:, sides[c]], woven[c][:].rearrange("p c u -> p (c u)").bitcast(BF16)
+                words[:].bitcast(FP8X4), scales[:, cols], woven[c][:].rearrange("p c u -> p (c u)").bitcast(BF16)
             )
-            nc.sync.dma_start(words_out[:, sides[c]], words[:].bitcast(I32))
+            nc.sync.dma_start(words_out[:, cols], words[:].bitcast(I32))
         for q in range(4):
             queue = nc.scalar if q % 2 == 0 else nc.sync
             queue.dma_start(scales_out[4 * q : 4 * q + 4, :], scales[32 * q : 32 * q + 4, :].bitcast(I32))

@@ -86,40 +86,37 @@ def tile_picked_idxput_min_lo_kernel(tc, xT, mem, w1, offs, slot, out_0, out_1, 
         x_codes, x_scales = codes[:, :S], exps[:, :S]
         w_codes, w_scales = [first_codes[:], codes[:, S:]], [first_exps[:], exps[:, S:]]
 
-        old_tiles = [sb.tile([P, n * H], F32, name="old%d" % i) for i, n in enumerate((1, 1, 2, 4))]
-        new_tiles = [sb.tile([P, n * H], F32, name="new%d" % i) for i, n in enumerate((1, 1, 2, 3, 1))]
-        place = {(0, 0): (0, 0), (0, 1): (1, 0), (1, 0): (2, 0), (1, 1): (2, H), (2, 0): (3, 0), (2, 1): (3, H), (3, 0): (3, S)}
+        old_t = sb.tile([P, 2 * PACK, H], F32, name="old_t")
+        new_t = sb.tile([P, 2 * PACK, H], F32, name="new_t")
+        row = {0: 0, 1: 2, 3: 4, 2: 6}
 
-        def old(t, first, count):
-            i, at = place.get((t, first // H), (3, S + H))
-            return old_tiles[i][:, at : at + count]
+        def rows_of(tile, pieces):
+            at = [row[t] + h for t, h in pieces]
+            step = at[1] - at[0] if len(at) > 1 else 1
+            return tile[:, at[0] : at[-1] + 1 : step, :]
 
-        def new(t, first, count):
-            i, at = place.get((t, first // H), (4, 0))
-            return new_tiles[i][:, at : at + count]
+        def run_of(tile, t, first, count):
+            at = row[t] * H + first
+            return tile[:].rearrange("p r h -> p (r h)")[:, at : at + count]
 
         pairs = sb.tile([P, 2, U, 2], BF16, name="pairs", align_bytes=64)
 
         def gather(engine, t, first, count):
-            copy_on(engine, old(t, first, count), win[t][:].indirect(slot_t[:, entries(first, count)]))
+            copy_on(engine, run_of(old_t, t, first, count), win[t][:].indirect(slot_t[:, entries(first, count)]))
 
         def smaller(*pieces):
-            t0, first0, count0 = pieces[0]
-            total = sum(piece[2] for piece in pieces)
-            y = ps.tile([P, total], F32, name="y%d_%d" % (t0, first0))
-            done = 0
-            for t, first, count in pieces:
+            y = ps.tile([P, len(pieces), H], F32, name="y%d_%d" % pieces[0], tag="y%d_%d" % (pieces[0][0], pieces[0][1] if pieces[0][0] else 0))
+            for c, (t, h) in enumerate(pieces):
                 rows = slice((t % 2) * P, (t % 2 + 1) * P)
-                cols = slice(first, first + count)
+                cols = slice(h * H, (h + 1) * H)
                 nc.tensor.matmul_mx(
-                    y[:, done : done + count], w_codes[t // 2][:, rows].bitcast(FP8X4), w_scales[t // 2][:, rows],
+                    y[:, c, :], w_codes[t // 2][:, rows].bitcast(FP8X4), w_scales[t // 2][:, rows],
                     x_codes[:, cols].bitcast(FP8X4), x_scales[:, cols], start=True, stop=True,
                 )
-                done = done + count
-            nc.vector.tensor_tensor(new(t0, first0, total), y[:], old(t0, first0, total), MIN)
+            nc.vector.tensor_tensor(rows_of(new_t, pieces), y[:], rows_of(old_t, pieces), MIN)
 
         def scatter(engine, t, first, count):
-            copy_on(engine, win[t][:].indirect(slot_t[:, entries(first, count)]), new(t, first, count))
+            copy_on(engine, win[t][:].indirect(slot_t[:, entries(first, count)]), run_of(new_t, t, first, count))
 
         def store(t):
             nc.sync.dma_start(out_rows[:, t, :], win[t][:])
@@ -129,26 +126,27 @@ def tile_picked_idxput_min_lo_kernel(tc, xT, mem, w1, offs, slot, out_0, out_1, 
 
         gather("scalar", 0, 0, H)
         gather("scalar", 0, H, H)
-        for first in (0, H):
-            smaller((0, first, H))
-            scatter("scalar", 0, first, H)
+        smaller((0, 0))
+        scatter("scalar", 0, 0, H)
+        gather("vector", 1, 0, S)
+        smaller((0, 1))
+        scatter("scalar", 0, H, H)
         store(0)
         round_early(0)
-        gather("vector", 1, 0, S)
-        smaller((1, 0, S))
+        smaller((1, 0))
+        scatter("scalar", 1, 0, H)
         gather("vector", 3, 0, S)
-        gather("vector", 2, 0, S)
-        smaller((3, H, H))
-        smaller((2, 0, H))
-        smaller((2, H, H), (3, 0, H))
-        for first in (0, H):
-            scatter("scalar", 1, first, H)
+        smaller((1, 1), (3, 1))
+        scatter("scalar", 3, H, H)
+        scatter("scalar", 1, H, H)
         store(1)
         round_early(1)
+        gather("vector", 2, 0, S)
+        smaller((2, 0))
+        smaller((3, 0), (2, 1))
         scatter("vector", 2, 0, S)
         store(2)
-        for first in (H, 0):
-            scatter("scalar", 3, first, H)
+        scatter("scalar", 3, 0, H)
         store(3)
 
         scales = sb.tile([P, U], U8, name="scales", align_bytes=64)

@@ -19,7 +19,10 @@ P = 128
 PACK = 4
 HALF = U // 2
 JOIN = 640
+LAST = 128
 H = S // 2
+Q = S // 4
+ORDER = (0, 1, 3, 2)
 GROUP = 16
 WEAVE = 96
 
@@ -47,7 +50,7 @@ def tile_picked_idxput_min_lo_kernel(tc, xT, mem, w1, offs, slot, out_0, out_1, 
             nc.sync.dma_start(x[j][:], x_rows[:, j, :])
         nc.sync.dma_start(w[:], w_rows)
         nc.sync.dma_start(slot_t[:], slot)
-        for t in (0, 1, 3, 2):
+        for t in ORDER:
             nc.sync.dma_start(win[t][:], mem_rows[:, t, :])
 
         def entries(first, count):
@@ -86,34 +89,32 @@ def tile_picked_idxput_min_lo_kernel(tc, xT, mem, w1, offs, slot, out_0, out_1, 
         x_codes, x_scales = codes[:, :S], exps[:, :S]
         w_codes, w_scales = [first_codes[:], codes[:, S:]], [first_exps[:], exps[:, S:]]
 
-        old_t = sb.tile([P, 2 * PACK, H], F32, name="old_t")
-        new_t = sb.tile([P, 2 * PACK, H], F32, name="new_t")
-        row = {0: 0, 1: 2, 3: 4, 2: 6}
-
-        def rows_of(tile, pieces):
-            at = [row[t] + h for t, h in pieces]
-            step = at[1] - at[0] if len(at) > 1 else 1
-            return tile[:, at[0] : at[-1] + 1 : step, :]
+        old_t = sb.tile([P, PACK * S], F32, name="old_t")
+        new_t = sb.tile([P, PACK * S], F32, name="new_t")
+        start = {t: i * S for i, t in enumerate(ORDER)}
 
         def run_of(tile, t, first, count):
-            at = row[t] * H + first
-            return tile[:].rearrange("p r h -> p (r h)")[:, at : at + count]
+            return tile[:, start[t] + first : start[t] + first + count]
 
         pairs = sb.tile([P, 2, U, 2], BF16, name="pairs", align_bytes=64)
 
         def gather(engine, t, first, count):
             copy_on(engine, run_of(old_t, t, first, count), win[t][:].indirect(slot_t[:, entries(first, count)]))
 
-        def smaller(*pieces):
-            y = ps.tile([P, len(pieces), H], F32, name="y%d_%d" % pieces[0], tag="y%d_%d" % (pieces[0][0], pieces[0][1] if pieces[0][0] else 0))
-            for c, (t, h) in enumerate(pieces):
+        def smaller(bank, *pieces):
+            t0, first0, count0 = pieces[0]
+            total = sum(piece[2] for piece in pieces)
+            y = ps.tile([P, total], F32, name="y%d_%d" % (t0, first0), tag=bank)
+            done = 0
+            for t, first, count in pieces:
                 rows = slice((t % 2) * P, (t % 2 + 1) * P)
-                cols = slice(h * H, (h + 1) * H)
+                cols = slice(first, first + count)
                 nc.tensor.matmul_mx(
-                    y[:, c, :], w_codes[t // 2][:, rows].bitcast(FP8X4), w_scales[t // 2][:, rows],
+                    y[:, done : done + count], w_codes[t // 2][:, rows].bitcast(FP8X4), w_scales[t // 2][:, rows],
                     x_codes[:, cols].bitcast(FP8X4), x_scales[:, cols], start=True, stop=True,
                 )
-            nc.vector.tensor_tensor(rows_of(new_t, pieces), y[:], rows_of(old_t, pieces), MIN)
+                done = done + count
+            nc.vector.tensor_tensor(run_of(new_t, t0, first0, total), y[:], run_of(old_t, t0, first0, total), MIN)
 
         def scatter(engine, t, first, count):
             copy_on(engine, win[t][:].indirect(slot_t[:, entries(first, count)]), run_of(new_t, t, first, count))
@@ -126,27 +127,27 @@ def tile_picked_idxput_min_lo_kernel(tc, xT, mem, w1, offs, slot, out_0, out_1, 
 
         gather("scalar", 0, 0, H)
         gather("scalar", 0, H, H)
-        smaller((0, 0))
+        smaller("a", (0, 0, H))
         scatter("scalar", 0, 0, H)
         gather("vector", 1, 0, S)
-        smaller((0, 1))
+        smaller("a", (0, H, H))
         scatter("scalar", 0, H, H)
         store(0)
         round_early(0)
-        smaller((1, 0))
+        smaller("b", (1, 0, H))
         scatter("scalar", 1, 0, H)
         gather("vector", 3, 0, S)
-        smaller((1, 1), (3, 1))
-        scatter("scalar", 3, H, H)
+        smaller("c", (1, H, H), (3, 0, Q))
+        scatter("scalar", 3, 0, Q)
         scatter("scalar", 1, H, H)
         store(1)
         round_early(1)
         gather("vector", 2, 0, S)
-        smaller((2, 0))
-        smaller((3, 0), (2, 1))
+        smaller("d", (2, Q, H), (2, Q + H, Q))
+        smaller("e", (3, Q, H), (3, Q + H, Q), (2, 0, Q))
         scatter("vector", 2, 0, S)
         store(2)
-        scatter("scalar", 3, 0, H)
+        scatter("scalar", 3, Q, S - Q)
         store(3)
 
         scales = sb.tile([P, U], U8, name="scales", align_bytes=64)
@@ -164,11 +165,12 @@ def tile_picked_idxput_min_lo_kernel(tc, xT, mem, w1, offs, slot, out_0, out_1, 
         nc.vector.tensor_copy(
             woven[1][:, : JOIN - HALF, :].bitcast(I32), pair_ints[:, :, HALF:JOIN].rearrange("p u c -> p c u")
         )
-        for c in range(2):
-            cols = slice(c * HALF, (c + 1) * HALF)
-            words = sb.tile([P, HALF], U32, name="words%d" % c, align_bytes=64)
+        for c, first, count in ((0, 0, HALF), (1, 0, HALF - LAST), (1, HALF - LAST, LAST)):
+            cols = slice(c * HALF + first, c * HALF + first + count)
+            words = sb.tile([P, count], U32, name="words%d_%d" % (c, first), align_bytes=64)
             nc.vector.quantize_mx(
-                words[:].bitcast(FP8X4), scales[:, cols], woven[c][:].rearrange("p c u -> p (c u)").bitcast(BF16)
+                words[:].bitcast(FP8X4), scales[:, cols],
+                woven[c][:, first : first + count, :].rearrange("p c u -> p (c u)").bitcast(BF16),
             )
             nc.sync.dma_start(words_out[:, cols], words[:].bitcast(I32))
         for q in range(4):

@@ -22,6 +22,7 @@ JOIN = 640
 LAST = 128
 H = S // 2
 Q = S // 4
+DEAL = 48
 ORDER = (0, 1, 3, 2)
 GROUP = 16
 WEAVE = 96
@@ -81,7 +82,9 @@ def tile_picked_idxput_min_lo_kernel(tc, xT, mem, w1, offs, slot, out_0, out_1, 
         wg = sb.tile([P, 2, P, PACK], BF16, name="wg", align_bytes=64)
         w_dealt = w[:].rearrange("p j (m t) -> p m j t", t=PACK)
         nc.vector.tensor_copy(wg[:].rearrange("p e m j -> p m j e"), w_dealt[:, :, :, 0:2])
-        nc.scalar.copy(late[:, 1].rearrange("p (e m) j -> p m j e", e=2), w_dealt[:, :, :, 2:4])
+        late_dealt = late[:, 1].rearrange("p (e m) j -> p m j e", e=2)
+        nc.vector.tensor_copy(late_dealt[:, :DEAL], w_dealt[:, :DEAL, :, 2:4])
+        nc.scalar.copy(late_dealt[:, DEAL:], w_dealt[:, DEAL:, :, 2:4])
         first_codes = sb.tile([P, 2 * P], U32, name="first_codes", align_bytes=64)
         first_exps = sb.tile([P, 2 * P], U8, name="first_exps", align_bytes=64)
         nc.vector.quantize_mx(first_codes[:].bitcast(FP8X4), first_exps[:], wg[:].rearrange("p e m j -> p (e m j)"))

@@ -18,8 +18,8 @@ COPY = mybir.ActivationFunctionType.Copy
 P = 128
 PACK = 4
 HALF = U // 2
-JOIN = 640
-LAST = 128
+JOIN = 704
+CUTS = (0, 256, 640, 896, U)
 H = S // 2
 Q = S // 4
 DEAL = 48
@@ -158,24 +158,20 @@ def tile_picked_idxput_min_lo_kernel(tc, xT, mem, w1, offs, slot, out_0, out_1, 
         scales_out = out_2[0].bitcast(I32)
         pair_words = pairs[:].rearrange("p u c e -> p u (c e)").bitcast(U32)
         pair_ints = pairs[:].rearrange("p u c e -> p u (c e)").bitcast(I32)
-        woven = [sb.tile([P, HALF, 2], U32, name="woven%d" % c, align_bytes=64) for c in range(2)]
-        for t in (3, 2):
-            nc.scalar.copy(pairs[:, 1, JOIN:, t % 2], win[t][:, JOIN:])
+        woven = sb.tile([P, U, 2], U32, name="woven", align_bytes=64)
         for t in (2, 3):
+            nc.scalar.copy(pairs[:, 1, JOIN:, t % 2], win[t][:, JOIN:])
             nc.vector.tensor_copy(pairs[:, 1, :JOIN, t % 2], win[t][:, :JOIN])
-        nc.scalar.copy(woven[1][:, JOIN - HALF :, :], pair_words[:, :, JOIN:].rearrange("p u c -> p c u"))
-        nc.vector.tensor_copy(woven[0][:].bitcast(I32), pair_ints[:, :, :HALF].rearrange("p u c -> p c u"))
-        nc.vector.tensor_copy(
-            woven[1][:, : JOIN - HALF, :].bitcast(I32), pair_ints[:, :, HALF:JOIN].rearrange("p u c -> p c u")
-        )
-        for c, first, count in ((0, 0, HALF), (1, 0, HALF - LAST), (1, HALF - LAST, LAST)):
-            cols = slice(c * HALF + first, c * HALF + first + count)
-            words = sb.tile([P, count], U32, name="words%d_%d" % (c, first), align_bytes=64)
+        nc.scalar.copy(woven[:, JOIN:, :], pair_words[:, :, JOIN:].rearrange("p u c -> p c u"))
+        for first, last in ((0, CUTS[1]), (CUTS[1], JOIN)):
+            nc.vector.tensor_copy(woven[:, first:last, :].bitcast(I32), pair_ints[:, :, first:last].rearrange("p u c -> p c u"))
+        for first, last in zip(CUTS, CUTS[1:]):
+            words = sb.tile([P, last - first], U32, name="words%d" % first, align_bytes=64)
             nc.vector.quantize_mx(
-                words[:].bitcast(FP8X4), scales[:, cols],
-                woven[c][:, first : first + count, :].rearrange("p c u -> p (c u)").bitcast(BF16),
+                words[:].bitcast(FP8X4), scales[:, first:last],
+                woven[:, first:last, :].rearrange("p c u -> p (c u)").bitcast(BF16),
             )
-            nc.sync.dma_start(words_out[:, cols], words[:].bitcast(I32))
+            nc.sync.dma_start(words_out[:, first:last], words[:].bitcast(I32))
         for q in range(4):
             queue = nc.scalar if q % 2 == 0 else nc.sync
             queue.dma_start(scales_out[4 * q : 4 * q + 4, :], scales[32 * q : 32 * q + 4, :].bitcast(I32))

@@ -19,7 +19,7 @@ P = 128
 PACK = 4
 HALF = U // 2
 JOIN = 704
-CUTS = (0, 256, 640, 896, U)
+CUTS = (0, 256, 640, U)
 H = S // 2
 Q = S // 4
 DEAL = 48
@@ -161,7 +161,9 @@ def tile_picked_idxput_min_lo_kernel(tc, xT, mem, w1, offs, slot, out_0, out_1, 
         woven = sb.tile([P, U, 2], U32, name="woven", align_bytes=64)
         for t in (2, 3):
             nc.scalar.copy(pairs[:, 1, JOIN:, t % 2], win[t][:, JOIN:])
-            nc.vector.tensor_copy(pairs[:, 1, :JOIN, t % 2], win[t][:, :JOIN])
+        nc.vector.tensor_copy(pairs[:, 1, :JOIN, 0], win[2][:, :JOIN])
+        for first, last in ((0, CUTS[1]), (CUTS[1], JOIN)):
+            nc.vector.tensor_copy(pairs[:, 1, first:last, 1], win[3][:, first:last])
         nc.scalar.copy(woven[:, JOIN:, :], pair_words[:, :, JOIN:].rearrange("p u c -> p c u"))
         for first, last in ((0, CUTS[1]), (CUTS[1], JOIN)):
             nc.vector.tensor_copy(woven[:, first:last, :].bitcast(I32), pair_ints[:, :, first:last].rearrange("p u c -> p c u"))

@@ -139,13 +139,15 @@ def tile_picked_idxput_min_lo_kernel(tc, xT, mem, w1, offs, slot, out_0, out_1, 
         round_early(0)
         smaller("b", (1, 0, H))
         scatter("scalar", 1, 0, H)
-        gather("vector", 3, 0, S)
+        gather("vector", 3, 0, Q)
+        gather("vector", 3, Q, S - Q)
         smaller("c", (1, H, H), (3, 0, Q))
         scatter("scalar", 3, 0, Q)
         scatter("scalar", 1, H, H)
         store(1)
         round_early(1)
-        gather("vector", 2, 0, S)
+        gather("vector", 2, Q, S - Q)
+        gather("vector", 2, 0, Q)
         smaller("d", (2, Q, H), (2, Q + H, Q))
         smaller("e", (3, Q, H), (3, Q + H, Q), (2, 0, Q))
         scatter("vector", 2, 0, S)

@@ -13,19 +13,21 @@ U16 = mybir.dt.uint16
 U8 = mybir.dt.uint8
 FP8X4 = mybir.dt.float8_e4m3fn_x4
 MIN = mybir.AluOpType.min
+MULT = mybir.AluOpType.mult
+ADD = mybir.AluOpType.add
 COPY = mybir.ActivationFunctionType.Copy
 
 P = 128
 PACK = 4
-HALF = U // 2
-JOIN = 704
-CUTS = (0, 256, 640, U)
+CUTS = (0, 384, 768, U)
 H = S // 2
 Q = S // 4
 DEAL = 48
-ORDER = (0, 1, 3, 2)
+A, B, C, D = 0, 2, 3, 1
+ORDER = (A, B, C, D)
+SHARE = 384
 GROUP = 16
-WEAVE = 96
+WEAVE = 160
 
 
 def tile_picked_idxput_min_lo_kernel(tc, xT, mem, w1, offs, slot, out_0, out_1, out_2):
@@ -63,57 +65,59 @@ def tile_picked_idxput_min_lo_kernel(tc, xT, mem, w1, offs, slot, out_0, out_1, 
             else:
                 nc.scalar.activation(dst, src, COPY)
 
-        picked = [sb.tile([P, PACK, H], BF16, name="picked%d" % h, align_bytes=64) for h in range(2)]
         x0 = sb.tile([P, T], BF16, name="x0_rounded", align_bytes=64)
         nc.scalar.copy(x0[:, : T // 4], x[0][:, : T // 4])
         nc.vector.tensor_copy(x0[:, T // 4 :], x[0][:, T // 4 :])
-        for j, window in enumerate([x0] + x[1:]):
-            for h, engine in enumerate(("vector", "scalar")):
-                copy_on(engine, picked[h][:, j, :], window[:].indirect(offs_t[:, entries(h * H, H)]))
-        early = sb.tile([P, H, PACK], BF16, name="early", align_bytes=64)
-        late = sb.tile([P, 2, H, PACK], BF16, name="late", align_bytes=64)
-        nc.vector.tensor_copy(early[:], picked[0][:].rearrange("p j s -> p s j"))
-        nc.vector.tensor_copy(late[:, 0, :WEAVE, :], picked[1][:, :, :WEAVE].rearrange("p j s -> p s j"))
-        nc.scalar.copy(late[:, 0, WEAVE:, :], picked[1][:, :, WEAVE:].rearrange("p j s -> p s j"))
-        codes = sb.tile([P, S + 2 * P], U32, name="codes", align_bytes=64)
-        exps = sb.tile([P, S + 2 * P], U8, name="exps", align_bytes=64)
-        nc.vector.quantize_mx(codes[:, :H].bitcast(FP8X4), exps[:, :H], early[:].rearrange("p c j -> p (c j)"))
+        picked = sb.tile([P, PACK, H], BF16, name="picked", align_bytes=64)
+        xg = sb.tile([P, S, PACK], BF16, name="xg", align_bytes=64)
+        for j in range(PACK):
+            nc.vector.tensor_copy(xg[:, :H, j], x[j][:].indirect(offs_t[:, entries(0, H)]))
+            window = x[j] if j else x0
+            nc.scalar.activation(picked[:, j, :], window[:].indirect(offs_t[:, entries(H, H)]), COPY)
+        nc.vector.tensor_copy(xg[:, H : H + WEAVE, :], picked[:, :, :WEAVE].rearrange("p j s -> p s j"))
+        nc.scalar.copy(xg[:, H + WEAVE :, :], picked[:, :, WEAVE:].rearrange("p j s -> p s j"))
+        x_codes = sb.tile([P, S], U32, name="x_codes", align_bytes=64)
+        x_scales = sb.tile([P, S], U8, name="x_scales", align_bytes=64)
+        nc.vector.quantize_mx(x_codes[:].bitcast(FP8X4), x_scales[:], xg[:].rearrange("p c j -> p (c j)"))
 
-        wg = sb.tile([P, 2, P, PACK], BF16, name="wg", align_bytes=64)
         w_dealt = w[:].rearrange("p j (m t) -> p m j t", t=PACK)
-        nc.vector.tensor_copy(wg[:].rearrange("p e m j -> p m j e"), w_dealt[:, :, :, 0:2])
-        late_dealt = late[:, 1].rearrange("p (e m) j -> p m j e", e=2)
-        nc.vector.tensor_copy(late_dealt[:, :DEAL], w_dealt[:, :DEAL, :, 2:4])
-        nc.scalar.copy(late_dealt[:, DEAL:], w_dealt[:, DEAL:, :, 2:4])
-        first_codes = sb.tile([P, 2 * P], U32, name="first_codes", align_bytes=64)
-        first_exps = sb.tile([P, 2 * P], U8, name="first_exps", align_bytes=64)
-        nc.vector.quantize_mx(first_codes[:].bitcast(FP8X4), first_exps[:], wg[:].rearrange("p e m j -> p (e m j)"))
-        nc.vector.quantize_mx(codes[:, H:].bitcast(FP8X4), exps[:, H:], late[:].rearrange("p a c j -> p (a c j)"))
-        x_codes, x_scales = codes[:, :S], exps[:, :S]
-        w_codes, w_scales = [first_codes[:], codes[:, S:]], [first_exps[:], exps[:, S:]]
+        wg = [sb.tile([P, 2, P, PACK], BF16, name="wg%d" % e, align_bytes=64) for e in range(2)]
+        w_codes = [sb.tile([P, 2 * P], U32, name="w_codes%d" % e, align_bytes=64) for e in range(2)]
+        w_scales = [sb.tile([P, 2 * P], U8, name="w_scales%d" % e, align_bytes=64) for e in range(2)]
+        nc.vector.tensor_copy(wg[0][:].rearrange("p e m j -> p m j e"), w_dealt[:, :, :, 0:4:2])
+        late_dealt = wg[1][:].rearrange("p e m j -> p m j e")
+        nc.vector.tensor_copy(late_dealt[:, :DEAL], w_dealt[:, :DEAL, :, 1:4:2])
+        nc.scalar.copy(late_dealt[:, DEAL:], w_dealt[:, DEAL:, :, 1:4:2])
+        for e in range(2):
+            nc.vector.quantize_mx(w_codes[e][:].bitcast(FP8X4), w_scales[e][:], wg[e][:].rearrange("p e m j -> p (e m j)"))
 
         old_t = sb.tile([P, PACK * S], F32, name="old_t")
         new_t = sb.tile([P, PACK * S], F32, name="new_t")
-        start = {t: i * S for i, t in enumerate(ORDER)}
+        pieces = [(A, 0, H), (B, 0, Q), (A, H, H), (B, Q, S - Q), (C, 0, S), (D, 0, S)]
+        start = {}
+        for t, first, count in pieces:
+            start[t, first] = sum(piece[2] for piece in pieces[: len(start)])
 
         def run_of(tile, t, first, count):
-            return tile[:, start[t] + first : start[t] + first + count]
+            base = max(key[1] for key in start if key[0] == t and key[1] <= first)
+            at = start[t, base] + first - base
+            return tile[:, at : at + count]
 
         pairs = sb.tile([P, 2, U, 2], BF16, name="pairs", align_bytes=64)
 
         def gather(engine, t, first, count):
             copy_on(engine, run_of(old_t, t, first, count), win[t][:].indirect(slot_t[:, entries(first, count)]))
 
-        def smaller(bank, *pieces):
-            t0, first0, count0 = pieces[0]
-            total = sum(piece[2] for piece in pieces)
+        def smaller(bank, *parts):
+            t0, first0, count0 = parts[0]
+            total = sum(part[2] for part in parts)
             y = ps.tile([P, total], F32, name="y%d_%d" % (t0, first0), tag=bank)
             done = 0
-            for t, first, count in pieces:
-                rows = slice((t % 2) * P, (t % 2 + 1) * P)
+            for t, first, count in parts:
+                rows = slice((t // 2) * P, (t // 2 + 1) * P)
                 cols = slice(first, first + count)
                 nc.tensor.matmul_mx(
-                    y[:, done : done + count], w_codes[t // 2][:, rows].bitcast(FP8X4), w_scales[t // 2][:, rows],
+                    y[:, done : done + count], w_codes[t % 2][:, rows].bitcast(FP8X4), w_scales[t % 2][:, rows],
                     x_codes[:, cols].bitcast(FP8X4), x_scales[:, cols], start=True, stop=True,
                 )
                 done = done + count
@@ -125,35 +129,40 @@ def tile_picked_idxput_min_lo_kernel(tc, xT, mem, w1, offs, slot, out_0, out_1, 
         def store(t):
             nc.sync.dma_start(out_rows[:, t, :], win[t][:])
 
-        def round_early(t):
-            nc.gpsimd.tensor_scalar(pairs[:, 0, :, t], win[t][:], 1.0, -0.0, mybir.AluOpType.mult, mybir.AluOpType.add)
+        def round_half(t, first, last):
+            nc.gpsimd.tensor_scalar(pairs[:, t // 2, first:last, t % 2], win[t][:, first:last], 1.0, -0.0, MULT, ADD)
 
-        gather("scalar", 0, 0, H)
-        gather("scalar", 0, H, H)
-        smaller("a", (0, 0, H))
-        scatter("scalar", 0, 0, H)
-        gather("vector", 1, 0, S)
-        smaller("a", (0, H, H))
-        scatter("scalar", 0, H, H)
-        store(0)
-        round_early(0)
-        smaller("b", (1, 0, H))
-        scatter("scalar", 1, 0, H)
-        gather("vector", 3, 0, Q)
-        gather("vector", 3, Q, S - Q)
-        smaller("c", (1, H, H), (3, 0, Q))
-        scatter("scalar", 3, 0, Q)
-        scatter("scalar", 1, H, H)
-        store(1)
-        round_early(1)
-        gather("vector", 2, Q, S - Q)
-        gather("vector", 2, 0, Q)
-        smaller("d", (2, Q, H), (2, Q + H, Q))
-        smaller("e", (3, Q, H), (3, Q + H, Q), (2, 0, Q))
-        scatter("vector", 2, 0, S)
-        store(2)
-        scatter("scalar", 3, Q, S - Q)
-        store(3)
+        def round_whole(t, first, last):
+            both = win[t][:, first:last].unsqueeze(2).to_broadcast([P, last - first, 2])
+            nc.gpsimd.tensor_scalar(pairs[:, t // 2, first:last, :], both, 1.0, -0.0, MULT, ADD)
+
+        gather("scalar", A, 0, H)
+        gather("scalar", A, H, H)
+        smaller("a", (A, 0, H))
+        scatter("scalar", A, 0, H)
+        gather("vector", B, 0, Q)
+        gather("vector", B, Q, S - Q)
+        smaller("b", (B, 0, Q), (A, H, H))
+        scatter("scalar", B, 0, Q)
+        scatter("scalar", A, H, H)
+        store(A)
+        round_whole(A, 0, U)
+        gather("vector", C, 0, S)
+        smaller("c", (B, Q, H), (B, Q + H, Q))
+        scatter("scalar", B, Q, S - Q)
+        store(B)
+        round_half(B, 0, SHARE)
+        round_whole(B, SHARE, U)
+        smaller("d", (C, 0, S))
+        gather("vector", D, 0, S)
+        scatter("vector", C, 0, Q)
+        smaller("e", (D, 0, S))
+        scatter("scalar", C, Q, S - Q)
+        store(C)
+        round_half(C, 0, SHARE)
+        nc.scalar.copy(pairs[:, C // 2, SHARE:, C % 2], win[C][:, SHARE:])
+        scatter("vector", D, 0, S)
+        store(D)
 
         scales = sb.tile([P, U], U8, name="scales", align_bytes=64)
         words_out = out_1[0].rearrange("p c r -> p (c r)").bitcast(I32)
@@ -161,14 +170,17 @@ def tile_picked_idxput_min_lo_kernel(tc, xT, mem, w1, offs, slot, out_0, out_1, 
         pair_words = pairs[:].rearrange("p u c e -> p u (c e)").bitcast(U32)
         pair_ints = pairs[:].rearrange("p u c e -> p u (c e)").bitcast(I32)
         woven = sb.tile([P, U, 2], U32, name="woven", align_bytes=64)
-        for t in (2, 3):
-            nc.scalar.copy(pairs[:, 1, JOIN:, t % 2], win[t][:, JOIN:])
-        nc.vector.tensor_copy(pairs[:, 1, :JOIN, 0], win[2][:, :JOIN])
-        for first, last in ((0, CUTS[1]), (CUTS[1], JOIN)):
-            nc.vector.tensor_copy(pairs[:, 1, first:last, 1], win[3][:, first:last])
-        nc.scalar.copy(woven[:, JOIN:, :], pair_words[:, :, JOIN:].rearrange("p u c -> p c u"))
-        for first, last in ((0, CUTS[1]), (CUTS[1], JOIN)):
-            nc.vector.tensor_copy(woven[:, first:last, :].bitcast(I32), pair_ints[:, :, first:last].rearrange("p u c -> p c u"))
+        stretches = list(zip(CUTS, CUTS[1:]))
+
+        def round_last(first, last):
+            nc.vector.tensor_copy(pairs[:, D // 2, first:last, D % 2], win[D][:, first:last])
+
+        round_last(*stretches[0])
+        round_last(*stretches[1])
+        nc.vector.tensor_copy(woven[:, : CUTS[1], :].bitcast(I32), pair_ints[:, :, : CUTS[1]].rearrange("p u c -> p c u"))
+        round_last(*stretches[2])
+        for first, last in stretches[1:]:
+            nc.scalar.copy(woven[:, first:last, :], pair_words[:, :, first:last].rearrange("p u c -> p c u"))
         for first, last in zip(CUTS, CUTS[1:]):
             words = sb.tile([P, last - first], U32, name="words%d" % first, align_bytes=64)
             nc.vector.quantize_mx(

@@ -22,10 +22,11 @@ PACK = 4
 CUTS = (0, 384, 768, U)
 H = S // 2
 Q = S // 4
-DEAL = 48
+DEAL = 28
 A, B, C, D = 0, 2, 3, 1
 ORDER = (A, B, C, D)
 SHARE = 384
+SPLIT = 160
 GROUP = 16
 WEAVE = 160
 
@@ -93,7 +94,7 @@ def tile_picked_idxput_min_lo_kernel(tc, xT, mem, w1, offs, slot, out_0, out_1, 
 
         old_t = sb.tile([P, PACK * S], F32, name="old_t")
         new_t = sb.tile([P, PACK * S], F32, name="new_t")
-        pieces = [(A, 0, H), (B, 0, Q), (A, H, H), (B, Q, S - Q), (C, 0, S), (D, 0, S)]
+        pieces = [(t, 0, S) for t in ORDER]
         start = {}
         for t, first, count in pieces:
             start[t, first] = sum(piece[2] for piece in pieces[: len(start)])
@@ -126,8 +127,8 @@ def tile_picked_idxput_min_lo_kernel(tc, xT, mem, w1, offs, slot, out_0, out_1, 
         def scatter(engine, t, first, count):
             copy_on(engine, win[t][:].indirect(slot_t[:, entries(first, count)]), run_of(new_t, t, first, count))
 
-        def store(t):
-            nc.sync.dma_start(out_rows[:, t, :], win[t][:])
+        def store(t, queue=nc.sync):
+            queue.dma_start(out_rows[:, t, :], win[t][:])
 
         def round_half(t, first, last):
             nc.gpsimd.tensor_scalar(pairs[:, t // 2, first:last, t % 2], win[t][:, first:last], 1.0, -0.0, MULT, ADD)
@@ -142,23 +143,25 @@ def tile_picked_idxput_min_lo_kernel(tc, xT, mem, w1, offs, slot, out_0, out_1, 
         scatter("scalar", A, 0, H)
         gather("vector", B, 0, Q)
         gather("vector", B, Q, S - Q)
-        smaller("b", (B, 0, Q), (A, H, H))
+        smaller("b", (A, H, H), (B, 0, Q))
         scatter("scalar", B, 0, Q)
         scatter("scalar", A, H, H)
         store(A)
         round_whole(A, 0, U)
-        gather("vector", C, 0, S)
-        smaller("c", (B, Q, H), (B, Q + H, Q))
+        gather("vector", C, 0, Q)
+        gather("vector", C, Q, S - Q)
+        smaller("c", (B, Q, H), (B, Q + H, Q), (C, 0, Q))
         scatter("scalar", B, Q, S - Q)
         store(B)
         round_half(B, 0, SHARE)
         round_whole(B, SHARE, U)
-        smaller("d", (C, 0, S))
-        gather("vector", D, 0, S)
-        scatter("vector", C, 0, Q)
-        smaller("e", (D, 0, S))
-        scatter("scalar", C, Q, S - Q)
-        store(C)
+        gather("vector", D, 0, Q)
+        gather("vector", D, Q, S - Q)
+        smaller("d", (C, Q, H), (C, Q + H, Q), (D, 0, Q))
+        smaller("e", (D, Q, H), (D, Q + H, Q))
+        scatter("vector", C, S - SPLIT, SPLIT)
+        scatter("scalar", C, 0, S - SPLIT)
+        store(C, nc.scalar)
         round_half(C, 0, SHARE)
         nc.scalar.copy(pairs[:, C // 2, SHARE:, C % 2], win[C][:, SHARE:])
         scatter("vector", D, 0, S)

@@ -19,10 +19,11 @@ COPY = mybir.ActivationFunctionType.Copy
 
 P = 128
 PACK = 4
+JOIN = 448
 CUTS = (0, 384, 768, U)
 H = S // 2
 Q = S // 4
-DEAL = 28
+DEAL = 48
 A, B, C, D = 0, 2, 3, 1
 ORDER = (A, B, C, D)
 SHARE = 384
@@ -127,8 +128,8 @@ def tile_picked_idxput_min_lo_kernel(tc, xT, mem, w1, offs, slot, out_0, out_1, 
         def scatter(engine, t, first, count):
             copy_on(engine, win[t][:].indirect(slot_t[:, entries(first, count)]), run_of(new_t, t, first, count))
 
-        def store(t, queue=nc.sync):
-            queue.dma_start(out_rows[:, t, :], win[t][:])
+        def store(t):
+            nc.sync.dma_start(out_rows[:, t, :], win[t][:])
 
         def round_half(t, first, last):
             nc.gpsimd.tensor_scalar(pairs[:, t // 2, first:last, t % 2], win[t][:, first:last], 1.0, -0.0, MULT, ADD)
@@ -161,7 +162,7 @@ def tile_picked_idxput_min_lo_kernel(tc, xT, mem, w1, offs, slot, out_0, out_1, 
         smaller("e", (D, Q, H), (D, Q + H, Q))
         scatter("vector", C, S - SPLIT, SPLIT)
         scatter("scalar", C, 0, S - SPLIT)
-        store(C, nc.scalar)
+        store(C)
         round_half(C, 0, SHARE)
         nc.scalar.copy(pairs[:, C // 2, SHARE:, C % 2], win[C][:, SHARE:])
         scatter("vector", D, 0, S)
@@ -173,16 +174,14 @@ def tile_picked_idxput_min_lo_kernel(tc, xT, mem, w1, offs, slot, out_0, out_1, 
         pair_words = pairs[:].rearrange("p u c e -> p u (c e)").bitcast(U32)
         pair_ints = pairs[:].rearrange("p u c e -> p u (c e)").bitcast(I32)
         woven = sb.tile([P, U, 2], U32, name="woven", align_bytes=64)
-        stretches = list(zip(CUTS, CUTS[1:]))
-
         def round_last(first, last):
             nc.vector.tensor_copy(pairs[:, D // 2, first:last, D % 2], win[D][:, first:last])
 
-        round_last(*stretches[0])
-        round_last(*stretches[1])
-        nc.vector.tensor_copy(woven[:, : CUTS[1], :].bitcast(I32), pair_ints[:, :, : CUTS[1]].rearrange("p u c -> p c u"))
-        round_last(*stretches[2])
-        for first, last in stretches[1:]:
+        round_last(0, JOIN)
+        round_last(JOIN, CUTS[2])
+        nc.vector.tensor_copy(woven[:, :JOIN, :].bitcast(I32), pair_ints[:, :, :JOIN].rearrange("p u c -> p c u"))
+        round_last(CUTS[2], U)
+        for first, last in ((JOIN, CUTS[2]), (CUTS[2], U)):
             nc.scalar.copy(woven[:, first:last, :], pair_words[:, :, first:last].rearrange("p u c -> p c u"))
         for first, last in zip(CUTS, CUTS[1:]):
             words = sb.tile([P, last - first], U32, name="words%d" % first, align_bytes=64)

@@ -191,5 +191,4 @@ def tile_picked_idxput_min_lo_kernel(tc, xT, mem, w1, offs, slot, out_0, out_1, 
             )
             nc.sync.dma_start(words_out[:, first:last], words[:].bitcast(I32))
         for q in range(4):
-            queue = nc.scalar if q % 2 == 0 else nc.sync
-            queue.dma_start(scales_out[4 * q : 4 * q + 4, :], scales[32 * q : 32 * q + 4, :].bitcast(I32))
+            nc.sync.dma_start(scales_out[4 * q : 4 * q + 4, :], scales[32 * q : 32 * q + 4, :].bitcast(I32))

@@ -27,6 +27,7 @@ DEAL = 48
 A, B, C, D = 0, 2, 3, 1
 ORDER = (A, B, C, D)
 SHARE = 384
+EDGE = 32
 SPLIT = 160
 GROUP = 16
 WEAVE = 160
@@ -148,14 +149,15 @@ def tile_picked_idxput_min_lo_kernel(tc, xT, mem, w1, offs, slot, out_0, out_1, 
         scatter("scalar", B, 0, Q)
         scatter("scalar", A, H, H)
         store(A)
-        round_whole(A, 0, U)
+        round_half(A, EDGE, U)
+        round_whole(A, 0, EDGE)
         gather("vector", C, 0, Q)
         gather("vector", C, Q, S - Q)
         smaller("c", (B, Q, H), (B, Q + H, Q), (C, 0, Q))
         scatter("scalar", B, Q, S - Q)
         store(B)
-        round_half(B, 0, SHARE)
-        round_whole(B, SHARE, U)
+        round_half(B, 0, U - EDGE)
+        round_whole(B, U - EDGE, U)
         gather("vector", D, 0, Q)
         gather("vector", D, Q, S - Q)
         smaller("d", (C, Q, H), (C, Q + H, Q), (D, 0, Q))

@@ -30,7 +30,7 @@ SHARE = 384
 EDGE = 32
 SPLIT = 160
 GROUP = 16
-WEAVE = 160
+WEAVE = 96
 
 
 def tile_picked_idxput_min_lo_kernel(tc, xT, mem, w1, offs, slot, out_0, out_1, out_2):
@@ -68,31 +68,34 @@ def tile_picked_idxput_min_lo_kernel(tc, xT, mem, w1, offs, slot, out_0, out_1, 
             else:
                 nc.scalar.activation(dst, src, COPY)
 
+        picked = [sb.tile([P, PACK, H], BF16, name="picked%d" % h, align_bytes=64) for h in range(2)]
         x0 = sb.tile([P, T], BF16, name="x0_rounded", align_bytes=64)
         nc.scalar.copy(x0[:, : T // 4], x[0][:, : T // 4])
         nc.vector.tensor_copy(x0[:, T // 4 :], x[0][:, T // 4 :])
-        picked = sb.tile([P, PACK, H], BF16, name="picked", align_bytes=64)
-        xg = sb.tile([P, S, PACK], BF16, name="xg", align_bytes=64)
-        for j in range(PACK):
-            nc.vector.tensor_copy(xg[:, :H, j], x[j][:].indirect(offs_t[:, entries(0, H)]))
-            window = x[j] if j else x0
-            nc.scalar.activation(picked[:, j, :], window[:].indirect(offs_t[:, entries(H, H)]), COPY)
-        nc.vector.tensor_copy(xg[:, H : H + WEAVE, :], picked[:, :, :WEAVE].rearrange("p j s -> p s j"))
-        nc.scalar.copy(xg[:, H + WEAVE :, :], picked[:, :, WEAVE:].rearrange("p j s -> p s j"))
-        x_codes = sb.tile([P, S], U32, name="x_codes", align_bytes=64)
-        x_scales = sb.tile([P, S], U8, name="x_scales", align_bytes=64)
-        nc.vector.quantize_mx(x_codes[:].bitcast(FP8X4), x_scales[:], xg[:].rearrange("p c j -> p (c j)"))
+        for j, window in enumerate([x0] + x[1:]):
+            for h, engine in enumerate(("vector", "scalar")):
+                copy_on(engine, picked[h][:, j, :], window[:].indirect(offs_t[:, entries(h * H, H)]))
+        early = sb.tile([P, H, PACK], BF16, name="early", align_bytes=64)
+        late = sb.tile([P, 2, H, PACK], BF16, name="late", align_bytes=64)
+        nc.vector.tensor_copy(early[:], picked[0][:].rearrange("p j s -> p s j"))
+        nc.vector.tensor_copy(late[:, 0, :WEAVE, :], picked[1][:, :, :WEAVE].rearrange("p j s -> p s j"))
+        nc.scalar.copy(late[:, 0, WEAVE:, :], picked[1][:, :, WEAVE:].rearrange("p j s -> p s j"))
+        codes = sb.tile([P, S + 2 * P], U32, name="codes", align_bytes=64)
+        exps = sb.tile([P, S + 2 * P], U8, name="exps", align_bytes=64)
+        nc.vector.quantize_mx(codes[:, :H].bitcast(FP8X4), exps[:, :H], early[:].rearrange("p c j -> p (c j)"))
 
+        wg = sb.tile([P, 2, P, PACK], BF16, name="wg", align_bytes=64)
         w_dealt = w[:].rearrange("p j (m t) -> p m j t", t=PACK)
-        wg = [sb.tile([P, 2, P, PACK], BF16, name="wg%d" % e, align_bytes=64) for e in range(2)]
-        w_codes = [sb.tile([P, 2 * P], U32, name="w_codes%d" % e, align_bytes=64) for e in range(2)]
-        w_scales = [sb.tile([P, 2 * P], U8, name="w_scales%d" % e, align_bytes=64) for e in range(2)]
-        nc.vector.tensor_copy(wg[0][:].rearrange("p e m j -> p m j e"), w_dealt[:, :, :, 0:4:2])
-        late_dealt = wg[1][:].rearrange("p e m j -> p m j e")
+        nc.vector.tensor_copy(wg[:].rearrange("p e m j -> p m j e"), w_dealt[:, :, :, 0:4:2])
+        late_dealt = late[:, 1].rearrange("p (e m) j -> p m j e", e=2)
         nc.vector.tensor_copy(late_dealt[:, :DEAL], w_dealt[:, :DEAL, :, 1:4:2])
         nc.scalar.copy(late_dealt[:, DEAL:], w_dealt[:, DEAL:, :, 1:4:2])
-        for e in range(2):
-            nc.vector.quantize_mx(w_codes[e][:].bitcast(FP8X4), w_scales[e][:], wg[e][:].rearrange("p e m j -> p (e m j)"))
+        first_codes = sb.tile([P, 2 * P], U32, name="first_codes", align_bytes=64)
+        first_exps = sb.tile([P, 2 * P], U8, name="first_exps", align_bytes=64)
+        nc.vector.quantize_mx(first_codes[:].bitcast(FP8X4), first_exps[:], wg[:].rearrange("p e m j -> p (e m j)"))
+        nc.vector.quantize_mx(codes[:, H:].bitcast(FP8X4), exps[:, H:], late[:].rearrange("p a c j -> p (a c j)"))
+        x_codes, x_scales = codes[:, :S], exps[:, :S]
+        w_codes, w_scales = [first_codes[:], codes[:, S:]], [first_exps[:], exps[:, S:]]
 
         old_t = sb.tile([P, PACK * S], F32, name="old_t")
         new_t = sb.tile([P, PACK * S], F32, name="new_t")

@@ -30,7 +30,6 @@ SHARE = 384
 EDGE = 32
 SPLIT = 160
 GROUP = 16
-WEAVE = 96
 
 
 def tile_picked_idxput_min_lo_kernel(tc, xT, mem, w1, offs, slot, out_0, out_1, out_2):
@@ -70,16 +69,15 @@ def tile_picked_idxput_min_lo_kernel(tc, xT, mem, w1, offs, slot, out_0, out_1, 
 
         picked = [sb.tile([P, PACK, H], BF16, name="picked%d" % h, align_bytes=64) for h in range(2)]
         x0 = sb.tile([P, T], BF16, name="x0_rounded", align_bytes=64)
-        nc.scalar.copy(x0[:, : T // 4], x[0][:, : T // 4])
-        nc.vector.tensor_copy(x0[:, T // 4 :], x[0][:, T // 4 :])
-        for j, window in enumerate([x0] + x[1:]):
+        nc.scalar.copy(x0[:], x[0][:])
+        for j in range(PACK):
             for h, engine in enumerate(("vector", "scalar")):
+                window = x0 if (j, h) == (0, 1) else x[j]
                 copy_on(engine, picked[h][:, j, :], window[:].indirect(offs_t[:, entries(h * H, H)]))
         early = sb.tile([P, H, PACK], BF16, name="early", align_bytes=64)
         late = sb.tile([P, 2, H, PACK], BF16, name="late", align_bytes=64)
         nc.vector.tensor_copy(early[:], picked[0][:].rearrange("p j s -> p s j"))
-        nc.vector.tensor_copy(late[:, 0, :WEAVE, :], picked[1][:, :, :WEAVE].rearrange("p j s -> p s j"))
-        nc.scalar.copy(late[:, 0, WEAVE:, :], picked[1][:, :, WEAVE:].rearrange("p j s -> p s j"))
+        nc.scalar.copy(late[:, 0], picked[1][:].rearrange("p j s -> p s j"))
         codes = sb.tile([P, S + 2 * P], U32, name="codes", align_bytes=64)
         exps = sb.tile([P, S + 2 * P], U8, name="exps", align_bytes=64)
         nc.vector.quantize_mx(codes[:, :H].bitcast(FP8X4), exps[:, :H], early[:].rearrange("p c j -> p (c j)"))

from contextlib import ExitStack

import concourse.mybir as mybir

K, T, S, N, U = 512, 1024, 512, 512, 1024
FLOPS = 2 * K * S * N

F32 = mybir.dt.float32
BF16 = mybir.dt.bfloat16
U32 = mybir.dt.uint32
I32 = mybir.dt.int32
U16 = mybir.dt.uint16
U8 = mybir.dt.uint8
FP8X4 = mybir.dt.float8_e4m3fn_x4
MIN = mybir.AluOpType.min
MULT = mybir.AluOpType.mult
ADD = mybir.AluOpType.add
COPY = mybir.ActivationFunctionType.Copy

P = 128
PACK = 4
JOIN = 448
CUTS = (0, 384, 768, U)
H = S // 2
Q = S // 4
DEAL = 48
A, B, C, D = 0, 2, 3, 1
ORDER = (A, B, C, D)
SHARE = 384
EDGE = 32
SPLIT = 160
GROUP = 16


def tile_picked_idxput_min_lo_kernel(tc, xT, mem, w1, offs, slot, out_0, out_1, out_2):
    nc = tc.nc
    with ExitStack() as ctx:
        sb = ctx.enter_context(tc.tile_pool(name="sb", bufs=1))
        ps = ctx.enter_context(tc.psum_pool(name="ps", bufs=1))

        offs_t = sb.tile([P, S // GROUP], U16, name="offs_t")
        slot_t = sb.tile([P, S // GROUP], U16, name="slot_t")
        x_rows = xT.rearrange("(p j) c -> p j c", j=PACK)
        w_rows = w1.rearrange("(p j) c -> p j c", j=PACK)
        mem_rows = mem.rearrange("(p t) c -> p t c", t=PACK)
        out_rows = out_0.rearrange("(p t) c -> p t c", t=PACK)

        x = [sb.tile([P, T], F32, name="x%d" % j) for j in range(PACK)]
        w = sb.tile([P, PACK, N], F32, name="w")
        win = [sb.tile([P, U], F32, name="win%d" % t) for t in range(PACK)]

        nc.sync.dma_start(x[0][:], x_rows[:, 0, :])
        nc.sync.dma_start(offs_t[:], offs)
        for j in range(1, PACK):
            nc.sync.dma_start(x[j][:], x_rows[:, j, :])
        nc.sync.dma_start(w[:], w_rows)
        nc.sync.dma_start(slot_t[:], slot)
        for t in ORDER:
            nc.sync.dma_start(win[t][:], mem_rows[:, t, :])

        def entries(first, count):
            return slice(first // GROUP, (first + count) // GROUP)

        def copy_on(engine, dst, src):
            if engine == "vector":
                nc.vector.tensor_copy(dst, src)
            else:
                nc.scalar.activation(dst, src, COPY)

        picked = [sb.tile([P, PACK, H], BF16, name="picked%d" % h, align_bytes=64) for h in range(2)]
        x0 = sb.tile([P, T], BF16, name="x0_rounded", align_bytes=64)
        nc.scalar.copy(x0[:], x[0][:])
        for j in range(PACK):
            for h, engine in enumerate(("vector", "scalar")):
                window = x0 if (j, h) == (0, 1) else x[j]
                copy_on(engine, picked[h][:, j, :], window[:].indirect(offs_t[:, entries(h * H, H)]))
        early = sb.tile([P, H, PACK], BF16, name="early", align_bytes=64)
        late = sb.tile([P, 2, H, PACK], BF16, name="late", align_bytes=64)
        nc.vector.tensor_copy(early[:], picked[0][:].rearrange("p j s -> p s j"))
        nc.scalar.copy(late[:, 0], picked[1][:].rearrange("p j s -> p s j"))
        codes = sb.tile([P, S + 2 * P], U32, name="codes", align_bytes=64)
        exps = sb.tile([P, S + 2 * P], U8, name="exps", align_bytes=64)
        nc.vector.quantize_mx(codes[:, :H].bitcast(FP8X4), exps[:, :H], early[:].rearrange("p c j -> p (c j)"))

        wg = sb.tile([P, 2, P, PACK], BF16, name="wg", align_bytes=64)
        w_dealt = w[:].rearrange("p j (m t) -> p m j t", t=PACK)
        nc.vector.tensor_copy(wg[:].rearrange("p e m j -> p m j e"), w_dealt[:, :, :, 0:4:2])
        late_dealt = late[:, 1].rearrange("p (e m) j -> p m j e", e=2)
        nc.vector.tensor_copy(late_dealt[:, :DEAL], w_dealt[:, :DEAL, :, 1:4:2])
        nc.scalar.copy(late_dealt[:, DEAL:], w_dealt[:, DEAL:, :, 1:4:2])
        first_codes = sb.tile([P, 2 * P], U32, name="first_codes", align_bytes=64)
        first_exps = sb.tile([P, 2 * P], U8, name="first_exps", align_bytes=64)
        nc.vector.quantize_mx(first_codes[:].bitcast(FP8X4), first_exps[:], wg[:].rearrange("p e m j -> p (e m j)"))
        nc.vector.quantize_mx(codes[:, H:].bitcast(FP8X4), exps[:, H:], late[:].rearrange("p a c j -> p (a c j)"))
        x_codes, x_scales = codes[:, :S], exps[:, :S]
        w_codes, w_scales = [first_codes[:], codes[:, S:]], [first_exps[:], exps[:, S:]]

        old_t = sb.tile([P, PACK * S], F32, name="old_t")
        new_t = sb.tile([P, PACK * S], F32, name="new_t")
        pieces = [(t, 0, S) for t in ORDER]
        start = {}
        for t, first, count in pieces:
            start[t, first] = sum(piece[2] for piece in pieces[: len(start)])

        def run_of(tile, t, first, count):
            base = max(key[1] for key in start if key[0] == t and key[1] <= first)
            at = start[t, base] + first - base
            return tile[:, at : at + count]

        pairs = sb.tile([P, 2, U, 2], BF16, name="pairs", align_bytes=64)

        def gather(engine, t, first, count):
            copy_on(engine, run_of(old_t, t, first, count), win[t][:].indirect(slot_t[:, entries(first, count)]))

        def smaller(bank, *parts):
            t0, first0, count0 = parts[0]
            total = sum(part[2] for part in parts)
            y = ps.tile([P, total], F32, name="y%d_%d" % (t0, first0), tag=bank)
            done = 0
            for t, first, count in parts:
                rows = slice((t // 2) * P, (t // 2 + 1) * P)
                cols = slice(first, first + count)
                nc.tensor.matmul_mx(
                    y[:, done : done + count], w_codes[t % 2][:, rows].bitcast(FP8X4), w_scales[t % 2][:, rows],
                    x_codes[:, cols].bitcast(FP8X4), x_scales[:, cols], start=True, stop=True,
                )
                done = done + count
            nc.vector.tensor_tensor(run_of(new_t, t0, first0, total), y[:], run_of(old_t, t0, first0, total), MIN)

        def scatter(engine, t, first, count):
            copy_on(engine, win[t][:].indirect(slot_t[:, entries(first, count)]), run_of(new_t, t, first, count))

        def store(t):
            nc.sync.dma_start(out_rows[:, t, :], win[t][:])

        def round_half(t, first, last):
            nc.gpsimd.tensor_scalar(pairs[:, t // 2, first:last, t % 2], win[t][:, first:last], 1.0, -0.0, MULT, ADD)

        def round_whole(t, first, last):
            both = win[t][:, first:last].unsqueeze(2).to_broadcast([P, last - first, 2])
            nc.gpsimd.tensor_scalar(pairs[:, t // 2, first:last, :], both, 1.0, -0.0, MULT, ADD)

        gather("scalar", A, 0, H)
        gather("scalar", A, H, H)
        smaller("a", (A, 0, H))
        scatter("scalar", A, 0, H)
        gather("vector", B, 0, Q)
        gather("vector", B, Q, S - Q)
        smaller("b", (A, H, H), (B, 0, Q))
        scatter("scalar", B, 0, Q)
        scatter("scalar", A, H, H)
        store(A)
        round_half(A, EDGE, U)
        round_whole(A, 0, EDGE)
        gather("vector", C, 0, Q)
        gather("vector", C, Q, S - Q)
        smaller("c", (B, Q, H), (B, Q + H, Q), (C, 0, Q))
        scatter("scalar", B, Q, S - Q)
        store(B)
        round_half(B, 0, U - EDGE)
        round_whole(B, U - EDGE, U)
        gather("vector", D, 0, Q)
        gather("vector", D, Q, S - Q)
        smaller("d", (C, Q, H), (C, Q + H, Q), (D, 0, Q))
        smaller("e", (D, Q, H), (D, Q + H, Q))
        scatter("vector", C, S - SPLIT, SPLIT)
        scatter("scalar", C, 0, S - SPLIT)
        store(C)
        round_half(C, 0, SHARE)
        nc.scalar.copy(pairs[:, C // 2, SHARE:, C % 2], win[C][:, SHARE:])
        scatter("vector", D, 0, S)
        store(D)

        scales = sb.tile([P, U], U8, name="scales", align_bytes=64)
        words_out = out_1[0].rearrange("p c r -> p (c r)").bitcast(I32)
        scales_out = out_2[0].bitcast(I32)
        pair_words = pairs[:].rearrange("p u c e -> p u (c e)").bitcast(U32)
        pair_ints = pairs[:].rearrange("p u c e -> p u (c e)").bitcast(I32)
        woven = sb.tile([P, U, 2], U32, name="woven", align_bytes=64)
        def round_last(first, last):
            nc.vector.tensor_copy(pairs[:, D // 2, first:last, D % 2], win[D][:, first:last])

        round_last(0, JOIN)
        round_last(JOIN, CUTS[2])
        nc.vector.tensor_copy(woven[:, :JOIN, :].bitcast(I32), pair_ints[:, :, :JOIN].rearrange("p u c -> p c u"))
        round_last(CUTS[2], U)
        for first, last in ((JOIN, CUTS[2]), (CUTS[2], U)):
            nc.scalar.copy(woven[:, first:last, :], pair_words[:, :, first:last].rearrange("p u c -> p c u"))
        for first, last in zip(CUTS, CUTS[1:]):
            words = sb.tile([P, last - first], U32, name="words%d" % first, align_bytes=64)
            nc.vector.quantize_mx(
                words[:].bitcast(FP8X4), scales[:, first:last],
                woven[:, first:last, :].rearrange("p c u -> p (c u)").bitcast(BF16),
            )
            nc.sync.dma_start(words_out[:, first:last], words[:].bitcast(I32))
        for q in range(4):
            nc.sync.dma_start(scales_out[4 * q : 4 * q + 4, :], scales[32 * q : 32 * q + 4, :].bitcast(I32))
